import numpy as np
import ml_dtypes


def mxq(x, axis, fmt="e4m3"):
    dtype, down = {"e4m3": (ml_dtypes.float8_e4m3fn, 7), "e5m2": (ml_dtypes.float8_e5m2, 14)}[fmt]
    v = np.moveaxis(np.asarray(x, np.float32).astype(ml_dtypes.bfloat16).astype(np.float64), axis, -1)
    blocks = v.reshape(v.shape[:-1] + (-1, 32))
    amax = np.abs(blocks).max(-1, keepdims=True)
    byte = np.maximum(np.where(amax > 0, np.frexp(amax)[1] - 1 + 127, 0) - down, 1)
    scale = np.exp2(byte - 127.0)
    codes = (blocks / scale).astype(np.float32).astype(dtype).astype(np.float64)
    return np.moveaxis((codes * scale).reshape(v.shape), -1, axis)


WIDE = False


def mx_kscale(k):
    if not WIDE:
        return np.ones(k)
    levels = np.array([10, -10, 5, -5, 0])
    if k % 512:
        return np.exp2(np.random.permutation(np.resize(levels, k // 32))).repeat(32)
    a = np.empty((k // 512, 16))
    for p in range(k // 512):
        a[p, :8] = np.random.permutation(np.resize(levels, 8))
        for g in range(8):
            far = levels[np.abs(levels - a[p, g]) >= 10]
            a[p, g + 8] = far[np.random.randint(len(far))]
    return np.exp2(a.ravel()).repeat(32)


BF16 = ml_dtypes.bfloat16


def bf(x):
    return np.asarray(x, np.float32).astype(BF16)


def f64(x):
    return np.asarray(x).astype(np.float64)


E2M1 = np.array([0.0, 0.5, 1.0, 1.5, 2.0, 3.0, 4.0, 6.0, -0.0, -0.5, -1.0, -1.5, -2.0, -3.0, -4.0, -6.0])


def pack_weight(w, fmt):
    k, n = w.shape
    w = f64(bf(w)).reshape(k // 32, 32, n)
    amax = np.abs(w).max(1)
    if fmt == "e4m3":
        byte = np.frexp(amax)[1] - 1 + 127 - 7
    else:
        mant, ex = np.frexp(amax / 6.0)
        byte = np.where(mant > 0.5, ex, ex - 1) + 127
    byte = np.clip(np.where(amax > 0, byte, 1), 1, 254)
    scaled = (w * np.exp2(127.0 - byte)[:, None, :]).reshape(k, n).astype(np.float32)
    by_word = np.ascontiguousarray(scaled.reshape(k // 512, 128, 4, n).transpose(0, 1, 3, 2))
    if fmt == "e4m3":
        words = by_word.astype(ml_dtypes.float8_e4m3fn).view(np.uint8)
    else:
        c = by_word.astype(ml_dtypes.float4_e2m1fn).view(np.uint8) & 0xF
        words = c[..., 0::2] | (c[..., 1::2] << 4)
    return np.ascontiguousarray(words), np.ascontiguousarray(byte.astype(np.uint8).reshape(k // 512, 16, n))


def unpack_weight(words, scales, fmt):
    g, p, n, _ = words.shape
    if fmt == "e4m3":
        vals = np.ascontiguousarray(words).view(ml_dtypes.float8_e4m3fn).astype(np.float64)
    else:
        nib = np.empty((g, p, n, 4), np.uint8)
        nib[..., 0::2] = words & 0xF
        nib[..., 1::2] = words >> 4
        vals = E2M1[nib]
    vals = vals * np.repeat(np.exp2(scales.astype(np.float64) - 127.0), 8, axis=1)[..., None]
    return vals.transpose(0, 1, 3, 2).reshape(g * 512, n)
def pack4(w):
    words, scales = pack_weight(w, "e2m1")
    return words.reshape(words.shape[0], 128, -1), scales


def unpack4(words, scales):
    return unpack_weight(words.reshape(words.shape[0], 128, -1, 2), scales, "e2m1")


def planes(Y):
    n, m = Y.shape
    b = f64(bf(Y)).reshape(n // 32, 32, m)
    amax = np.abs(b).max(1)
    byte = np.clip(np.where(amax > 0, np.frexp(amax)[1] - 1 + 127 - 7, 1), 1, 254)
    codes = (b * np.exp2(127.0 - byte)[:, None, :]).reshape(n, m).astype(np.float32).astype(ml_dtypes.float8_e4m3fn).view(np.uint8)
    words = codes.reshape(n // 512, 128, 4, m).transpose(0, 1, 3, 2)
    return np.ascontiguousarray(words), np.ascontiguousarray(byte.astype(np.uint8).reshape(n // 512, 16, m))


QUERIES, QTOK, DOCS, DTOK, K = 128, 4, 1024, 8, 1024
ROWS = QUERIES * QTOK
COLS = DOCS * DTOK


def setup_inputs():
    s = mx_kscale(K)
    x = np.random.randn(QUERIES, QTOK, K) * s
    w_adapt = 0.47 / np.sqrt(K) * np.random.randn(K, K) / s[:, None] * s[None, :]
    w_proj = 0.35 / np.sqrt(K) * np.random.randn(K, K) / s[:, None] * s[None, :]
    docs = np.random.randn(K, COLS) / np.sqrt(K) / s[:, None]
    docs_words, docs_scales = pack4(docs)
    doc_weight = np.exp(0.7 * np.random.randn(DOCS)) / QTOK
    return {"x": bf(x), "w_adapt": bf(w_adapt), "w_proj": bf(w_proj),
            "docs_words": docs_words, "docs_scales": docs_scales, "doc_weight": bf(doc_weight)}


def reference(x, w_adapt, w_proj, docs_words, docs_scales, doc_weight):
    x = f64(x).reshape(ROWS, K)
    h = x + np.maximum(mxq(x, 1) @ mxq(f64(w_adapt), 0), 0.0)
    r = h + (mxq(h, 1) @ mxq(f64(w_proj), 0))
    sim = mxq(r, 1) @ unpack4(docs_words, docs_scales)
    best = sim.reshape(QUERIES, QTOK, DOCS, DTOK).max(axis=3)
    y = best.sum(axis=1) * f64(doc_weight)
    Y = y.T
    words, scales = planes(Y)
    return y, words, scales

@@ -1,0 +1,587 @@
+from contextlib import ExitStack
+
+import concourse.mybir as mybir
+from concourse.masks import make_identity
+
+F32 = mybir.dt.float32
+BF16 = mybir.dt.bfloat16
+I32 = mybir.dt.int32
+U32 = mybir.dt.uint32
+U8 = mybir.dt.uint8
+FP8X4 = mybir.dt.float8_e4m3fn_x4
+FP4X4 = mybir.dt.float4_e2m1fn_x4
+ALU = mybir.AluOpType
+ACT = mybir.ActivationFunctionType
+AXIS_X = mybir.AxisListType.X
+
+P = 128
+QTOK, DOCS, DTOK, K = 4, 1024, 8, 1024
+COLS = DOCS * DTOK
+G = K // 512
+BANK = 512
+CHUNKS = COLS // BANK
+CHUNK_DOCS = BANK // DTOK
+
+FLOPS = 2 * 512 * K * (K + K + COLS)
+
+VEC_SHARE = 60
+
+
+def tile_residual_query_maxsim_k1_kernel(
+    tc, x, w_adapt, w_proj, docs_words, docs_scales, doc_weight, out_0, out_1, out_2
+):
+    nc = tc.nc
+    with ExitStack() as ctx:
+        sb = ctx.enter_context(tc.tile_pool(name="sb", bufs=1))
+        ps = ctx.enter_context(tc.psum_pool(name="ps", bufs=1))
+        ctx.enter_context(tc.manual_schedule())
+
+        def keep(name, width, dtype):
+            return sb.tile([P, width], dtype, name=name, align_bytes=64)
+
+        banks = [ps.tile([P, BANK], F32, name="bank%d" % b) for b in range(8)]
+        ident = keep("ident", P, F32)
+        warm_in = keep("warm_in", 8, F32)
+        warm_out = keep("warm_out", 8, F32)
+        weights = (w_adapt, w_proj)
+        ident16 = keep("ident16", P, BF16)
+        w_raw = [[keep("w_raw%d%d" % (w, g), 4096, BF16) for g in range(G)] for w in range(2)]
+        w_grp = [[[keep("w_grp%d%d%d" % (w, g, h), 2048, BF16) for h in range(G)] for g in range(G)] for w in range(2)]
+        w_code = [[[keep("w_code%d%d%d" % (w, g, h), 512, U32) for h in range(G)] for g in range(G)] for w in range(2)]
+        w_scale = [[[keep("w_scale%d%d%d" % (w, g, h), 512, U8) for h in range(G)] for g in range(G)] for w in range(2)]
+        x_raw = [keep("x_raw%d" % n, 2 * K, BF16) for n in range(2)]
+        x_t = [keep("x_t%d" % i, K, BF16) for i in range(QTOK)]
+        z1 = {i: keep("z_%d" % i, K, F32) for i in range(1, QTOK)}
+        z2 = z1
+        h32 = [keep("h32_%d" % i, K, F32) for i in range(QTOK)]
+        h16 = [keep("h16_%d" % i, K, BF16) for i in range(QTOK)]
+        r16 = h16
+        x_code = [keep("x_code%d" % i, 256, U32) for i in range(QTOK)]
+        x_scale = [keep("x_scale%d" % i, 256, U8) for i in range(QTOK)]
+        h_code = [keep("h_code%d" % i, 256, U32) for i in range(QTOK)]
+        h_scale = [keep("h_scale%d" % i, 256, U8) for i in range(QTOK)]
+        r_code = x_code
+        r_scale = x_scale
+        d_word = keep("d_word", G * 2 * COLS, U8)
+        d_scale = keep("d_scale", G * COLS, U8)
+        d_weight = keep("d_weight", DOCS, BF16)
+        best = [keep("best%d" % i, DOCS, F32) for i in range(QTOK)]
+        sum01 = keep("sum01", DOCS, F32)
+        sum012 = sum01
+        total = sum01
+        y32 = keep("y32", DOCS, F32)
+        y16 = keep("y16", DOCS, BF16)
+        y_t = keep("y_t", DOCS, BF16)
+        y_code = keep("y_code", 256, U32)
+        y_scale = keep("y_scale", 256, U8)
+
+        def half(tile, h):
+            n = tile.shape[1] // 2
+            return tile[:, h * n : (h + 1) * n]
+
+        def by_word(ap):
+            return ap.rearrange("p (a t) -> p a t", t=4)
+
+        def bank_by_word(b):
+            return banks[b][:].rearrange("p (t a) -> p a t", t=4)
+
+        def load_w(w, g, lo, hi):
+            nc.sync.dma_start(
+                out=w_raw[w][g][:].rearrange("p (j c) -> p j c", j=4)[:, :, lo:hi],
+                in_=weights[w][512 * g : 512 * (g + 1), lo:hi].rearrange("(p j) c -> p j c", j=4),
+            )
+
+        def load_x(n):
+            nc.sync.dma_start(
+                out=x_raw[n][:].rearrange("p (i k) -> p i k", i=2), in_=x[:, 2 * n : 2 * n + 2, :]
+            )
+
+        d_word3 = d_word[:].rearrange("p (g n) -> p g n", g=G)
+        d_scale3 = d_scale[:].rearrange("p (g n) -> p g n", g=G)
+
+        def load_doc_words(c0, c1):
+            cols = slice(2 * BANK * c0, 2 * BANK * c1)
+            nc.sync.dma_start(
+                out=d_word3[:, :, cols].bitcast(I32),
+                in_=docs_words[:, :, cols].rearrange("g p n -> p g n").bitcast(I32),
+            )
+
+        def load_doc_scales(c0, c1):
+            cols = slice(BANK * c0, BANK * c1)
+            for r in range(4):
+                nc.sync.dma_start(
+                    out=d_scale3[r:P:32, :, cols].bitcast(I32),
+                    in_=docs_scales[:, r:16:4, cols].rearrange("g q n -> q g n").bitcast(I32),
+                )
+
+        def grouped(w, g, h):
+            return w_grp[w][g][h][:].rearrange("p (t m j) -> p t m j", t=4, j=4)
+
+        def weave(engine, w, g, h, m0, m1):
+            src = w_raw[w][g][:].rearrange("p (j h m t) -> p h t m j", j=4, h=G, t=4)[:, h, :, m0:m1, :]
+            dst = grouped(w, g, h)[:, :, m0:m1, :]
+            if engine == "V":
+                nc.vector.tensor_copy(out=dst, in_=src)
+            else:
+                nc.scalar.copy(out=dst, in_=src)
+
+        def weave_pe(w, g, h, e, b):
+            src = w_raw[w][g][:].rearrange("p (j c) -> p c j", j=4)
+            dst = banks[b][:].bitcast(BF16).rearrange("p (t m j) -> p m t j", t=4, j=4)
+            for s in range(2):
+                c0 = 512 * h + 256 * e + 128 * s
+                nc.tensor.matmul(
+                    out=dst[:, 32 * s : 32 * (s + 1), :, :], lhsT=ident16[:], rhs=src[:, c0 : c0 + 128, :],
+                    start=True, stop=True,
+                )
+
+        def weave_out(engine, w, g, h, e, b):
+            dst = grouped(w, g, h)[:, :, 64 * e : 64 * (e + 1), :]
+            src = banks[b][:].bitcast(BF16).rearrange("p (t m j) -> p t m j", t=4, j=4)
+            if engine == "V":
+                nc.vector.tensor_copy(out=dst, in_=src)
+            else:
+                nc.scalar.copy(out=dst, in_=src)
+
+        def quantize(code, scale, src):
+            nc.vector.quantize_mx(out=code.bitcast(FP8X4), scales=scale, in_=src)
+
+        def quantize_w(w, g, h):
+            quantize(w_code[w][g][h][:], w_scale[w][g][h][:], w_grp[w][g][h][:])
+
+        def turn(b, slot, words):
+            for u in range(2):
+                col = (2 * slot + u) * P
+                nc.tensor.transpose(banks[b][:, col : col + P], words[:, u:256:2], ident[:])
+
+        def turn_x(i, b):
+            words = half(x_raw[i // 2], i % 2).bitcast(F32)
+            for g in range(G):
+                turn(b, g, words[:, 256 * g : 256 * (g + 1)])
+
+        def copy_x(i, b):
+            nc.scalar.copy(
+                out=x_t[i][:].bitcast(F32).rearrange("p (g a u) -> p g a u", g=G, u=2),
+                in_=banks[b][:].rearrange("p (g u a) -> p g a u", g=G, u=2),
+            )
+
+        def project(w, h, code, scale, b):
+            for t in range(4):
+                cols = slice(P * t, P * (t + 1))
+                for g in range(G):
+                    nc.tensor.matmul_mx(
+                        out=banks[b][:, cols],
+                        lhsT=w_code[w][g][h][:, cols].bitcast(FP8X4),
+                        lhsT_scale=w_scale[w][g][h][:, cols],
+                        rhs=half(code, g).bitcast(FP8X4),
+                        rhs_scale=half(scale, g),
+                        start=(g == 0),
+                        stop=(g == G - 1),
+                    )
+
+        def stage1(i, h, b):
+            project(0, h, x_code[i], x_scale[i], b)
+
+        def stage2(i, h, b):
+            project(1, h, h_code[i], h_scale[i], b)
+
+        def h_on_vector(i, h, b):
+            nc.vector.scalar_tensor_tensor(
+                out=by_word(half(h32[i], h)), in0=bank_by_word(b), scalar=0.0,
+                in1=by_word(half(x_t[i], h)), op0=ALU.max, op1=ALU.add,
+            )
+
+        def r_on_vector(i, h, b):
+            nc.vector.tensor_tensor(
+                out=by_word(half(r16[i], h)), in0=bank_by_word(b), in1=by_word(half(h32[i], h)), op=ALU.add
+            )
+
+        def relu_out(i, h, b):
+            nc.scalar.activation(out=by_word(half(z1[i], h)), in_=bank_by_word(b), func=ACT.Relu)
+
+        def copy_out(i, h, b):
+            nc.scalar.copy(out=by_word(half(z2[i], h)), in_=bank_by_word(b))
+
+        def pool_op(dst, a, c, op, lo, hi):
+            for s in range(lo, hi, 256):
+                cols = slice(s, min(s + 256, hi))
+                nc.gpsimd.tensor_tensor(out=dst[:, cols], in0=a[:, cols], in1=c[:, cols], op=op)
+
+        def h_on_pool(i, h):
+            pool_op(h32[i], z1[i], x_t[i], ALU.add, 512 * h, 512 * (h + 1))
+
+        def r_on_pool(i, h):
+            pool_op(r16[i], z2[i], h32[i], ALU.add, 512 * h, 512 * (h + 1))
+
+        def round_h(i, h):
+            nc.scalar.copy(out=half(h16[i], h), in_=half(h32[i], h))
+
+        def round_h_on_vector(i):
+            nc.vector.tensor_copy(out=h16[i][:], in_=h32[i][:])
+
+        def quantize_x(i):
+            quantize(x_code[i][:], x_scale[i][:], x_t[i][:])
+
+        def quantize_h(i):
+            quantize(h_code[i][:], h_scale[i][:], h16[i][:])
+
+        def quantize_r(i):
+            quantize(r_code[i][:], r_scale[i][:], r16[i][:])
+
+        def score(i, c, b):
+            for g in range(G):
+                nc.tensor.matmul_mx(
+                    out=banks[b][:],
+                    lhsT=half(r_code[i], g).bitcast(FP8X4),
+                    lhsT_scale=half(r_scale[i], g),
+                    rhs=d_word3[:, g, 2 * BANK * c : 2 * BANK * (c + 1)].bitcast(FP4X4),
+                    rhs_scale=d_scale3[:, g, BANK * c : BANK * (c + 1)],
+                    start=(g == 0),
+                    stop=(g == G - 1),
+                )
+
+        def reduce_max(i, c, b):
+            nc.vector.tensor_reduce(
+                out=best[i][:, CHUNK_DOCS * c : CHUNK_DOCS * (c + 1)],
+                in_=banks[b][:].rearrange("p (d j) -> p d j", j=DTOK),
+                axis=AXIS_X,
+                op=ALU.max,
+            )
+
+        def finish_on_pool(lo, hi):
+            pool_op(total, sum012, best[3], ALU.add, lo, hi)
+            pool_op(y32, total, d_weight, ALU.mult, lo, hi)
+
+        def round_y(lo, hi):
+            nc.scalar.copy(out=y16[:, lo:hi], in_=y32[:, lo:hi])
+
+        def add_best(i, lo, hi):
+            pool_op(sum01, best[0] if i == 1 else sum01, best[i], ALU.add, lo, hi)
+
+        def quantize_r_half(i, h):
+            quantize(half(r_code[i], h), half(r_scale[i], h), half(r16[i], h))
+
+        def round_h_vec(i, h):
+            nc.vector.tensor_copy(out=half(h16[i], h), in_=half(h32[i], h))
+
+        def round_h_pool(i, h):
+            nc.gpsimd.tensor_scalar(
+                out=half(h16[i], h), in0=half(h32[i], h), scalar1=1.0, scalar2=0.0, op0=ALU.mult, op1=ALU.add
+            )
+
+        def finish_on_vector(lo, hi):
+            last = slice(lo, hi)
+            nc.vector.tensor_tensor(out=total[:, last], in0=sum012[:, last], in1=best[3][:, last], op=ALU.add)
+            nc.vector.tensor_tensor(out=y16[:, last], in0=total[:, last], in1=d_weight[:, last], op=ALU.mult)
+            nc.vector.tensor_tensor(out=y32[:, last], in0=total[:, last], in1=d_weight[:, last], op=ALU.mult)
+
+        def load_weight_row():
+            nc.sync.dma_start(out=d_weight[:], in_=doc_weight.partition_broadcast(P))
+
+        def store_scales(q):
+            y_scale3 = y_scale[:].rearrange("p (g m) -> p g m", g=G)
+            queue = nc.sync if q % 2 else nc.scalar
+            queue.dma_start(
+                out=out_2[:, 4 * q : 4 * q + 4, :].rearrange("g r m -> r g m").bitcast(I32),
+                in_=y_scale3[32 * q : 32 * q + 4, :, :].bitcast(I32),
+            )
+
+        def setup(with_pe):
+            nc.vector.memset(warm_in[:], 0.0)
+            nc.scalar.activation(out=warm_out[:], in_=warm_in[:], func=ACT.Relu)
+            make_identity(nc, ident[:])
+            if with_pe:
+                make_identity(nc, ident16[:])
+            nc.vector.memset(d_scale[:].bitcast(I32), 0)
+
+        def store_y(lo, hi):
+            nc.sync.dma_start(out=out_0[:, lo:hi], in_=y32[:, lo:hi])
+
+        def turn_y(g, b):
+            turn(b, 0, half(y16, g).bitcast(F32))
+
+        def copy_y(g, b):
+            nc.scalar.copy(
+                out=half(y_t, g).bitcast(F32).rearrange("p (a u) -> p a u", u=2),
+                in_=banks[b][:, : 2 * P].rearrange("p (u a) -> p a u", u=2),
+            )
+
+        def quantize_y(g):
+            quantize(half(y_code, g), half(y_scale, g), half(y_t, g))
+
+        def store_codes(g):
+            nc.sync.dma_start(
+                out=out_1[g].rearrange("p m t -> p (m t)").bitcast(I32), in_=half(y_code, g).bitcast(I32)
+            )
+
+        setup(0)
+        load_w(0, 0, 0, 512)
+        load_w(0, 0, 512, 1024)
+        load_x(0)
+        load_w(0, 1, 0, 1024)
+        load_x(1)
+        load_w(1, 0, 0, 512)
+        load_w(1, 1, 0, 512)
+        load_w(1, 0, 512, 1024)
+        load_w(1, 1, 512, 1024)
+        weave("S", 0, 0, 0, 64, 128)
+        weave("V", 0, 0, 0, 0, 64)
+        load_doc_scales(0, 4)
+        weave("S", 0, 0, 1, 64, 128)
+        weave("V", 0, 0, 1, 0, 64)
+        quantize_w(0, 0, 0)
+        turn_x(0, 0)
+        quantize_w(0, 0, 1)
+        turn_x(1, 1)
+        copy_x(0, 0)
+        quantize_x(0)
+        copy_x(1, 1)
+        weave("V", 0, 1, 0, 0, 64)
+        weave("S", 0, 1, 0, 64, 128)
+        weave("V", 0, 1, 1, 0, 64)
+        turn_x(2, 2)
+        weave("S", 0, 1, 1, 64, 128)
+        quantize_w(0, 1, 0)
+        stage1(0, 0, 3)
+        load_doc_words(0, 2)
+        weave("V", 1, 0, 0, 0, 64)
+        copy_x(2, 2)
+        quantize_w(0, 1, 1)
+        weave("S", 1, 0, 0, 64, 128)
+        stage1(0, 1, 4)
+        quantize_x(1)
+        load_doc_words(2, 4)
+        quantize_x(2)
+        weave("V", 1, 1, 0, 0, 64)
+        weave("S", 1, 1, 0, 64, 128)
+        stage1(2, 1, 5)
+        load_doc_scales(4, 8)
+        h_on_vector(0, 0, 3)
+        stage1(1, 0, 6)
+        weave("V", 1, 0, 1, 0, 64)
+        weave("S", 1, 0, 1, 64, 128)
+        stage1(2, 0, 7)
+        quantize_w(1, 0, 0)
+        turn_x(3, 0)
+        quantize_w(1, 1, 0)
+        round_h(0, 0)
+        load_doc_words(4, 6)
+        h_on_vector(0, 1, 4)
+        stage1(1, 1, 1)
+        load_doc_words(6, 8)
+        copy_x(3, 0)
+        weave("V", 1, 1, 1, 0, 80)
+        round_h(0, 1)
+        load_doc_scales(8, 16)
+        quantize_x(3)
+        weave("S", 1, 1, 1, 80, 128)
+        quantize_h(0)
+        stage1(3, 0, 2)
+        quantize_w(1, 0, 1)
+        relu_out(2, 1, 5)
+        stage2(0, 0, 3)
+        quantize_w(1, 1, 1)
+        stage2(0, 1, 4)
+        h_on_vector(1, 0, 6)
+        h_on_pool(2, 1)
+        load_doc_words(8, 10)
+        r_on_vector(0, 0, 3)
+        load_doc_words(10, 12)
+        stage1(3, 1, 0)
+        round_h(1, 0)
+        r_on_vector(0, 1, 4)
+        relu_out(3, 0, 2)
+        quantize_r_half(0, 0)
+        round_h(2, 1)
+        load_doc_words(12, 14)
+        quantize_r_half(0, 1)
+        h_on_vector(1, 1, 1)
+        score(0, 0, 5)
+        relu_out(2, 0, 7)
+        score(0, 1, 6)
+        reduce_max(0, 0, 5)
+        round_h(1, 1)
+        load_doc_words(14, 16)
+        score(0, 2, 3)
+        h_on_pool(2, 0)
+        relu_out(3, 1, 0)
+        score(0, 3, 4)
+        load_weight_row()
+        quantize_h(1)
+        reduce_max(0, 1, 6)
+        score(0, 4, 2)
+        reduce_max(0, 2, 3)
+        h_on_pool(3, 0)
+        score(0, 5, 1)
+        round_h(2, 0)
+        reduce_max(0, 3, 4)
+        stage2(1, 1, 7)
+        reduce_max(0, 4, 2)
+        stage2(1, 0, 5)
+        h_on_pool(3, 1)
+        reduce_max(0, 5, 1)
+        round_h(3, 0)
+        score(0, 6, 0)
+        r_on_vector(1, 0, 5)
+        score(0, 7, 6)
+        r_on_vector(1, 1, 7)
+        score(0, 8, 3)
+        quantize_h(2)
+        score(0, 9, 4)
+        quantize_r(1)
+        reduce_max(0, 6, 0)
+        score(0, 10, 2)
+        reduce_max(0, 7, 6)
+        score(0, 11, 1)
+        reduce_max(0, 8, 3)
+        score(1, 0, 5)
+        reduce_max(0, 9, 4)
+        score(1, 1, 7)
+        reduce_max(0, 10, 2)
+        score(1, 2, 0)
+        reduce_max(0, 11, 1)
+        score(1, 3, 6)
+        reduce_max(1, 0, 5)
+        score(1, 4, 3)
+        reduce_max(1, 1, 7)
+        stage2(2, 1, 4)
+        reduce_max(1, 2, 0)
+        score(1, 5, 2)
+        copy_out(2, 1, 4)
+        reduce_max(1, 3, 6)
+        stage2(2, 0, 1)
+        reduce_max(1, 4, 3)
+        score(1, 6, 5)
+        reduce_max(1, 5, 2)
+        copy_out(2, 0, 1)
+        score(1, 7, 7)
+        round_h(3, 1)
+        reduce_max(1, 6, 5)
+        r_on_pool(2, 0)
+        score(1, 8, 0)
+        reduce_max(1, 7, 7)
+        score(1, 9, 4)
+        reduce_max(1, 8, 0)
+        score(1, 10, 6)
+        r_on_pool(2, 1)
+        reduce_max(1, 9, 4)
+        score(1, 11, 3)
+        reduce_max(1, 10, 6)
+        score(0, 12, 2)
+        quantize_h(3)
+        score(0, 13, 1)
+        reduce_max(1, 11, 3)
+        add_best(1, 0, 512)
+        score(0, 14, 5)
+        reduce_max(0, 12, 2)
+        stage2(3, 1, 7)
+        reduce_max(0, 13, 1)
+        reduce_max(0, 14, 5)
+        score(0, 15, 0)
+        stage2(3, 0, 4)
+        reduce_max(0, 15, 0)
+        score(1, 12, 6)
+        quantize_r(2)
+        copy_out(3, 0, 4)
+        score(1, 13, 3)
+        copy_out(3, 1, 7)
+        reduce_max(1, 12, 6)
+        r_on_pool(3, 0)
+        score(1, 14, 2)
+        reduce_max(1, 13, 3)
+        score(1, 15, 1)
+        reduce_max(1, 14, 2)
+        score(2, 0, 5)
+        r_on_pool(3, 1)
+        reduce_max(1, 15, 1)
+        score(2, 1, 0)
+        reduce_max(2, 0, 5)
+        score(2, 2, 4)
+        reduce_max(2, 1, 0)
+        score(2, 3, 7)
+        reduce_max(2, 2, 4)
+        score(2, 4, 6)
+        quantize_r(3)
+        reduce_max(2, 3, 7)
+        score(2, 5, 3)
+        reduce_max(2, 4, 6)
+        score(2, 6, 2)
+        reduce_max(2, 5, 3)
+        score(2, 7, 1)
+        reduce_max(2, 6, 2)
+        score(2, 8, 5)
+        reduce_max(2, 7, 1)
+        add_best(2, 0, 512)
+        score(2, 9, 0)
+        reduce_max(2, 8, 5)
+        score(2, 10, 4)
+        reduce_max(2, 9, 0)
+        score(2, 11, 7)
+        add_best(1, 512, 1024)
+        reduce_max(2, 10, 4)
+        score(2, 12, 6)
+        reduce_max(2, 11, 7)
+        score(2, 13, 3)
+        reduce_max(2, 12, 6)
+        score(2, 14, 2)
+        reduce_max(2, 13, 3)
+        score(2, 15, 1)
+        reduce_max(2, 14, 2)
+        score(3, 0, 5)
+        reduce_max(2, 15, 1)
+        add_best(2, 512, 1024)
+        score(3, 1, 0)
+        reduce_max(3, 0, 5)
+        score(3, 2, 4)
+        reduce_max(3, 1, 0)
+        score(3, 3, 7)
+        reduce_max(3, 2, 4)
+        score(3, 4, 6)
+        reduce_max(3, 3, 7)
+        score(3, 5, 3)
+        reduce_max(3, 4, 6)
+        score(3, 6, 2)
+        finish_on_pool(0, 256)
+        reduce_max(3, 5, 3)
+        score(3, 7, 1)
+        reduce_max(3, 6, 2)
+        score(3, 8, 5)
+        reduce_max(3, 7, 1)
+        score(3, 9, 0)
+        reduce_max(3, 8, 5)
+        score(3, 10, 4)
+        finish_on_pool(256, 512)
+        reduce_max(3, 9, 0)
+        score(3, 11, 7)
+        reduce_max(3, 10, 4)
+        score(3, 12, 6)
+        reduce_max(3, 11, 7)
+        score(3, 13, 3)
+        finish_on_pool(512, 704)
+        store_y(0, 512)
+        reduce_max(3, 12, 6)
+        score(3, 14, 2)
+        reduce_max(3, 13, 3)
+        score(3, 15, 1)
+        finish_on_pool(704, 832)
+        reduce_max(3, 14, 2)
+        round_y(512, 704)
+        round_y(0, 256)
+        reduce_max(3, 15, 1)
+        round_y(256, 512)
+        turn_y(0, 5)
+        round_y(704, 832)
+        finish_on_vector(832, 1024)
+        copy_y(0, 5)
+        turn_y(1, 0)
+        quantize_y(0)
+        store_y(832, 1024)
+        store_y(512, 832)
+        store_codes(0)
+        copy_y(1, 0)
+        quantize_y(1)
+        store_codes(1)
+        store_scales(2)
+        store_scales(3)
+        store_scales(0)
+        store_scales(1)

@@ -24,7 +24,7 @@ CHUNK_DOCS = BANK // DTOK
 
 FLOPS = 2 * 512 * K * (K + K + COLS)
 
-VEC_SHARE = 60
+ZT = []
 
 
 def tile_residual_query_maxsim_k1_kernel(
@@ -51,7 +51,7 @@ def tile_residual_query_maxsim_k1_kernel(
         w_scale = [[[keep("w_scale%d%d%d" % (w, g, h), 512, U8) for h in range(G)] for g in range(G)] for w in range(2)]
         x_raw = [keep("x_raw%d" % n, 2 * K, BF16) for n in range(2)]
         x_t = [keep("x_t%d" % i, K, BF16) for i in range(QTOK)]
-        z1 = {i: keep("z_%d" % i, K, F32) for i in range(1, QTOK)}
+        z1 = {i: keep("z_%d" % i, K, F32) for i in ZT}
         z2 = z1
         h32 = [keep("h32_%d" % i, K, F32) for i in range(QTOK)]
         h16 = [keep("h16_%d" % i, K, BF16) for i in range(QTOK)]
@@ -69,6 +69,9 @@ def tile_residual_query_maxsim_k1_kernel(
         sum01 = keep("sum01", DOCS, F32)
         sum012 = sum01
         total = sum01
+        upper = [keep("upper%d" % n, 256, F32) for n in range(4)]
+        four = [keep("four%d" % n, 1024, F32) for n in range(2)]
+        two = [keep("two%d" % n, 512, F32) for n in range(2)]
         y32 = keep("y32", DOCS, F32)
         y16 = keep("y16", DOCS, BF16)
         y_t = keep("y_t", DOCS, BF16)
@@ -248,6 +251,51 @@ def tile_residual_query_maxsim_k1_kernel(
                 op=ALU.max,
             )
 
+        def copy_upper(n, b):
+            nc.scalar.copy(
+                out=upper[n % 4][:].rearrange("p (d j) -> p d j", j=4),
+                in_=banks[b][:].rearrange("p (d j) -> p d j", j=DTOK)[:, :, 4:],
+            )
+
+        def max_to_four(n, q, s, b):
+            nc.vector.tensor_tensor(
+                out=four[q % 2][:, 256 * s : 256 * (s + 1)].rearrange("p (d j) -> p d j", j=4),
+                in0=banks[b][:].rearrange("p (d j) -> p d j", j=DTOK)[:, :, :4],
+                in1=upper[n % 4][:].rearrange("p (d j) -> p d j", j=4),
+                op=ALU.max,
+            )
+
+        def max_to_two(q, count):
+            src = four[q % 2][:, : 256 * count].rearrange("p (d j) -> p d j", j=4)
+            nc.vector.tensor_tensor(
+                out=two[q % 2][:, : 128 * count].rearrange("p (d j) -> p d j", j=2),
+                in0=src[:, :, :2], in1=src[:, :, 2:], op=ALU.max,
+            )
+
+        def max_to_one(q, count, i, c):
+            src = two[q % 2][:, : 128 * count].rearrange("p (d j) -> p d j", j=2)
+            nc.vector.tensor_tensor(
+                out=best[i][:, CHUNK_DOCS * c : CHUNK_DOCS * (c + count)],
+                in0=src[:, :, 0], in1=src[:, :, 1], op=ALU.max,
+            )
+
+        def add_on_vector(i, lo, hi):
+            first = best[0] if i == 1 else sum01
+            nc.vector.tensor_tensor(out=sum01[:, lo:hi], in0=first[:, lo:hi], in1=best[i][:, lo:hi], op=ALU.add)
+
+        def weigh(lo, hi):
+            nc.vector.tensor_tensor(out=y32[:, lo:hi], in0=sum01[:, lo:hi], in1=d_weight[:, lo:hi], op=ALU.mult)
+
+        def weigh_rounded(lo, hi):
+            nc.vector.tensor_tensor(out=y16[:, lo:hi], in0=sum01[:, lo:hi], in1=d_weight[:, lo:hi], op=ALU.mult)
+
+        def store_scales_of(g, q):
+            queue = nc.sync if q % 2 else nc.scalar
+            queue.dma_start(
+                out=out_2[g, 4 * q : 4 * q + 4, :].bitcast(I32),
+                in_=half(y_scale, g)[32 * q : 32 * q + 4, :].bitcast(I32),
+            )
+
         def finish_on_pool(lo, hi):
             pool_op(total, sum012, best[3], ALU.add, lo, hi)
             pool_op(y32, total, d_weight, ALU.mult, lo, hi)
@@ -315,273 +363,363 @@ def tile_residual_query_maxsim_k1_kernel(
             )
 
         setup(0)
-        load_w(0, 0, 0, 512)
+        load_w(0, 1, 512, 1024)
+        load_w(1, 0, 0, 512)
         load_w(0, 0, 512, 1024)
         load_x(0)
-        load_w(0, 1, 0, 1024)
+        load_w(0, 0, 0, 512)
         load_x(1)
-        load_w(1, 0, 0, 512)
-        load_w(1, 1, 0, 512)
-        load_w(1, 0, 512, 1024)
+        load_w(0, 1, 0, 512)
         load_w(1, 1, 512, 1024)
+        load_w(1, 1, 0, 512)
+        weave("S", 0, 1, 1, 56, 128)
+        load_w(1, 0, 512, 1024)
+        weave("V", 1, 0, 0, 0, 48)
+        weave("S", 1, 0, 0, 48, 128)
+        load_doc_scales(0, 8)
+        weave("V", 0, 0, 1, 0, 64)
+        weave("S", 0, 0, 1, 64, 128)
+        weave("V", 0, 1, 1, 0, 56)
+        turn_x(1, 0)
+        quantize_w(0, 1, 1)
+        turn_x(0, 1)
+        quantize_w(0, 0, 1)
+        copy_x(1, 0)
+        quantize_w(1, 0, 0)
         weave("S", 0, 0, 0, 64, 128)
         weave("V", 0, 0, 0, 0, 64)
-        load_doc_scales(0, 4)
-        weave("S", 0, 0, 1, 64, 128)
-        weave("V", 0, 0, 1, 0, 64)
-        quantize_w(0, 0, 0)
-        turn_x(0, 0)
-        quantize_w(0, 0, 1)
-        turn_x(1, 1)
-        copy_x(0, 0)
-        quantize_x(0)
-        copy_x(1, 1)
-        weave("V", 0, 1, 0, 0, 64)
-        weave("S", 0, 1, 0, 64, 128)
-        weave("V", 0, 1, 1, 0, 64)
         turn_x(2, 2)
-        weave("S", 0, 1, 1, 64, 128)
-        quantize_w(0, 1, 0)
-        stage1(0, 0, 3)
-        load_doc_words(0, 2)
-        weave("V", 1, 0, 0, 0, 64)
-        copy_x(2, 2)
-        quantize_w(0, 1, 1)
-        weave("S", 1, 0, 0, 64, 128)
-        stage1(0, 1, 4)
         quantize_x(1)
-        load_doc_words(2, 4)
+        copy_x(0, 1)
+        quantize_w(0, 0, 0)
+        turn_x(3, 3)
+        copy_x(2, 2)
+        load_doc_words(0, 2)
+        quantize_x(0)
+        weave("V", 0, 1, 0, 0, 56)
+        weave("S", 0, 1, 0, 56, 128)
+        stage1(1, 1, 4)
         quantize_x(2)
-        weave("V", 1, 1, 0, 0, 64)
-        weave("S", 1, 1, 0, 64, 128)
-        stage1(2, 1, 5)
-        load_doc_scales(4, 8)
-        h_on_vector(0, 0, 3)
-        stage1(1, 0, 6)
-        weave("V", 1, 0, 1, 0, 64)
-        weave("S", 1, 0, 1, 64, 128)
+        load_doc_words(2, 4)
+        weave("V", 1, 1, 1, 0, 72)
+        stage1(0, 1, 5)
+        copy_x(3, 3)
+        quantize_w(0, 1, 0)
+        weave("S", 1, 1, 1, 72, 128)
+        load_doc_words(4, 8)
+        stage1(0, 0, 6)
+        weave("V", 1, 1, 0, 0, 48)
+        h_on_vector(0, 1, 5)
         stage1(2, 0, 7)
-        quantize_w(1, 0, 0)
-        turn_x(3, 0)
-        quantize_w(1, 1, 0)
-        round_h(0, 0)
-        load_doc_words(4, 6)
-        h_on_vector(0, 1, 4)
-        stage1(1, 1, 1)
-        load_doc_words(6, 8)
-        copy_x(3, 0)
-        weave("V", 1, 1, 1, 0, 80)
-        round_h(0, 1)
+        weave("S", 1, 1, 0, 48, 128)
+        h_on_vector(0, 0, 6)
         load_doc_scales(8, 16)
+        stage1(2, 1, 0)
+        h_on_vector(1, 1, 4)
+        stage1(1, 0, 1)
         quantize_x(3)
-        weave("S", 1, 1, 1, 80, 128)
-        quantize_h(0)
-        stage1(3, 0, 2)
-        quantize_w(1, 0, 1)
-        relu_out(2, 1, 5)
-        stage2(0, 0, 3)
+        round_h(0, 1)
         quantize_w(1, 1, 1)
-        stage2(0, 1, 4)
-        h_on_vector(1, 0, 6)
-        h_on_pool(2, 1)
-        load_doc_words(8, 10)
-        r_on_vector(0, 0, 3)
-        load_doc_words(10, 12)
-        stage1(3, 1, 0)
-        round_h(1, 0)
-        r_on_vector(0, 1, 4)
-        relu_out(3, 0, 2)
-        quantize_r_half(0, 0)
-        round_h(2, 1)
-        load_doc_words(12, 14)
-        quantize_r_half(0, 1)
-        h_on_vector(1, 1, 1)
-        score(0, 0, 5)
-        relu_out(2, 0, 7)
-        score(0, 1, 6)
-        reduce_max(0, 0, 5)
+        stage1(3, 0, 2)
+        round_h(0, 0)
+        h_on_vector(1, 0, 1)
+        stage1(3, 1, 3)
+        weave("S", 1, 0, 1, 48, 128)
+        quantize_w(1, 1, 0)
+        load_doc_words(8, 12)
+        quantize_h(0)
+        weave("V", 1, 0, 1, 0, 48)
+        stage2(0, 0, 5)
+        h_on_vector(2, 1, 0)
+        load_doc_words(12, 16)
         round_h(1, 1)
-        load_doc_words(14, 16)
-        score(0, 2, 3)
-        h_on_pool(2, 0)
-        relu_out(3, 1, 0)
-        score(0, 3, 4)
+        quantize_w(1, 0, 1)
+        round_h(1, 0)
+        round_h(2, 1)
         load_weight_row()
+        stage2(0, 1, 6)
         quantize_h(1)
-        reduce_max(0, 1, 6)
-        score(0, 4, 2)
-        reduce_max(0, 2, 3)
-        h_on_pool(3, 0)
-        score(0, 5, 1)
+        r_on_vector(0, 0, 5)
+        stage2(1, 0, 4)
+        r_on_vector(0, 1, 6)
+        stage2(1, 1, 1)
+        quantize_r_half(0, 0)
+        quantize_r_half(0, 1)
+        h_on_vector(3, 1, 3)
+        score(0, 0, 0)
+        h_on_vector(2, 0, 7)
+        score(0, 1, 5)
+        copy_upper(0, 0)
+        h_on_vector(3, 0, 2)
+        score(0, 2, 6)
         round_h(2, 0)
-        reduce_max(0, 3, 4)
-        stage2(1, 1, 7)
-        reduce_max(0, 4, 2)
-        stage2(1, 0, 5)
-        h_on_pool(3, 1)
-        reduce_max(0, 5, 1)
+        max_to_four(0, 0, 0, 0)
+        score(0, 3, 3)
+        copy_upper(1, 5)
+        r_on_vector(1, 1, 1)
         round_h(3, 0)
-        score(0, 6, 0)
-        r_on_vector(1, 0, 5)
-        score(0, 7, 6)
-        r_on_vector(1, 1, 7)
-        score(0, 8, 3)
-        quantize_h(2)
-        score(0, 9, 4)
-        quantize_r(1)
-        reduce_max(0, 6, 0)
-        score(0, 10, 2)
-        reduce_max(0, 7, 6)
-        score(0, 11, 1)
-        reduce_max(0, 8, 3)
-        score(1, 0, 5)
-        reduce_max(0, 9, 4)
-        score(1, 1, 7)
-        reduce_max(0, 10, 2)
-        score(1, 2, 0)
-        reduce_max(0, 11, 1)
-        score(1, 3, 6)
-        reduce_max(1, 0, 5)
-        score(1, 4, 3)
-        reduce_max(1, 1, 7)
-        stage2(2, 1, 4)
-        reduce_max(1, 2, 0)
-        score(1, 5, 2)
-        copy_out(2, 1, 4)
-        reduce_max(1, 3, 6)
-        stage2(2, 0, 1)
-        reduce_max(1, 4, 3)
-        score(1, 6, 5)
-        reduce_max(1, 5, 2)
-        copy_out(2, 0, 1)
-        score(1, 7, 7)
+        score(0, 4, 7)
+        max_to_four(1, 0, 1, 5)
         round_h(3, 1)
-        reduce_max(1, 6, 5)
-        r_on_pool(2, 0)
-        score(1, 8, 0)
-        reduce_max(1, 7, 7)
-        score(1, 9, 4)
-        reduce_max(1, 8, 0)
-        score(1, 10, 6)
-        r_on_pool(2, 1)
-        reduce_max(1, 9, 4)
-        score(1, 11, 3)
-        reduce_max(1, 10, 6)
-        score(0, 12, 2)
+        quantize_h(2)
+        score(0, 5, 2)
+        r_on_vector(1, 0, 4)
+        copy_upper(2, 6)
+        stage2(2, 0, 0)
+        copy_upper(3, 3)
         quantize_h(3)
-        score(0, 13, 1)
-        reduce_max(1, 11, 3)
-        add_best(1, 0, 512)
-        score(0, 14, 5)
-        reduce_max(0, 12, 2)
-        stage2(3, 1, 7)
-        reduce_max(0, 13, 1)
-        reduce_max(0, 14, 5)
-        score(0, 15, 0)
-        stage2(3, 0, 4)
-        reduce_max(0, 15, 0)
-        score(1, 12, 6)
+        copy_upper(4, 7)
+        max_to_four(2, 0, 2, 6)
+        score(0, 6, 1)
+        copy_upper(5, 2)
+        max_to_four(3, 0, 3, 3)
+        r_on_vector(2, 0, 0)
+        stage2(2, 1, 5)
+        copy_upper(6, 1)
+        quantize_r(1)
+        score(0, 7, 4)
+        max_to_four(4, 1, 0, 7)
+        max_to_four(5, 1, 1, 2)
+        stage2(3, 1, 6)
+        r_on_vector(2, 1, 5)
+        copy_upper(7, 4)
+        score(1, 0, 3)
+        max_to_two(0, 4)
+        score(1, 1, 0)
+        max_to_four(6, 1, 2, 1)
+        copy_upper(8, 3)
+        max_to_four(7, 1, 3, 4)
+        score(1, 2, 7)
         quantize_r(2)
-        copy_out(3, 0, 4)
-        score(1, 13, 3)
-        copy_out(3, 1, 7)
-        reduce_max(1, 12, 6)
-        r_on_pool(3, 0)
-        score(1, 14, 2)
-        reduce_max(1, 13, 3)
-        score(1, 15, 1)
-        reduce_max(1, 14, 2)
-        score(2, 0, 5)
-        r_on_pool(3, 1)
-        reduce_max(1, 15, 1)
-        score(2, 1, 0)
-        reduce_max(2, 0, 5)
-        score(2, 2, 4)
-        reduce_max(2, 1, 0)
-        score(2, 3, 7)
-        reduce_max(2, 2, 4)
-        score(2, 4, 6)
+        copy_upper(9, 0)
+        max_to_two(1, 4)
+        score(1, 3, 2)
+        copy_upper(10, 7)
+        max_to_four(8, 2, 0, 3)
+        score(1, 4, 5)
+        max_to_one(1, 4, 0, 4)
+        copy_upper(11, 2)
+        max_to_four(9, 2, 1, 0)
+        score(1, 5, 1)
+        max_to_four(10, 2, 2, 7)
+        copy_upper(12, 5)
+        max_to_one(0, 4, 0, 0)
+        score(1, 6, 4)
+        max_to_four(11, 2, 3, 2)
+        copy_upper(13, 1)
+        r_on_vector(3, 1, 6)
+        score(1, 7, 3)
+        copy_upper(14, 4)
+        max_to_four(12, 3, 0, 5)
+        score(2, 0, 0)
+        max_to_two(2, 4)
+        copy_upper(15, 3)
+        score(2, 1, 7)
+        max_to_four(13, 3, 1, 1)
+        copy_upper(16, 0)
+        max_to_four(14, 3, 2, 4)
+        score(2, 2, 2)
+        max_to_four(15, 3, 3, 3)
+        copy_upper(17, 7)
+        max_to_four(16, 4, 0, 0)
+        stage2(3, 0, 6)
+        max_to_four(17, 4, 1, 7)
+        copy_upper(18, 2)
+        max_to_two(3, 4)
+        score(2, 3, 5)
+        r_on_vector(3, 0, 6)
+        score(2, 4, 1)
+        copy_upper(19, 5)
+        max_to_four(18, 4, 2, 2)
+        score(2, 5, 4)
+        max_to_one(2, 4, 1, 0)
+        copy_upper(20, 1)
+        max_to_four(19, 4, 3, 5)
+        score(2, 6, 3)
         quantize_r(3)
-        reduce_max(2, 3, 7)
-        score(2, 5, 3)
-        reduce_max(2, 4, 6)
-        score(2, 6, 2)
-        reduce_max(2, 5, 3)
-        score(2, 7, 1)
-        reduce_max(2, 6, 2)
-        score(2, 8, 5)
-        reduce_max(2, 7, 1)
-        add_best(2, 0, 512)
-        score(2, 9, 0)
-        reduce_max(2, 8, 5)
-        score(2, 10, 4)
-        reduce_max(2, 9, 0)
-        score(2, 11, 7)
-        add_best(1, 512, 1024)
-        reduce_max(2, 10, 4)
-        score(2, 12, 6)
-        reduce_max(2, 11, 7)
-        score(2, 13, 3)
-        reduce_max(2, 12, 6)
-        score(2, 14, 2)
-        reduce_max(2, 13, 3)
-        score(2, 15, 1)
-        reduce_max(2, 14, 2)
-        score(3, 0, 5)
-        reduce_max(2, 15, 1)
-        add_best(2, 512, 1024)
-        score(3, 1, 0)
-        reduce_max(3, 0, 5)
-        score(3, 2, 4)
-        reduce_max(3, 1, 0)
-        score(3, 3, 7)
-        reduce_max(3, 2, 4)
-        score(3, 4, 6)
-        reduce_max(3, 3, 7)
-        score(3, 5, 3)
-        reduce_max(3, 4, 6)
-        score(3, 6, 2)
-        finish_on_pool(0, 256)
-        reduce_max(3, 5, 3)
-        score(3, 7, 1)
-        reduce_max(3, 6, 2)
-        score(3, 8, 5)
-        reduce_max(3, 7, 1)
-        score(3, 9, 0)
-        reduce_max(3, 8, 5)
-        score(3, 10, 4)
-        finish_on_pool(256, 512)
-        reduce_max(3, 9, 0)
-        score(3, 11, 7)
-        reduce_max(3, 10, 4)
-        score(3, 12, 6)
-        reduce_max(3, 11, 7)
-        score(3, 13, 3)
-        finish_on_pool(512, 704)
-        store_y(0, 512)
-        reduce_max(3, 12, 6)
-        score(3, 14, 2)
-        reduce_max(3, 13, 3)
-        score(3, 15, 1)
-        finish_on_pool(704, 832)
-        reduce_max(3, 14, 2)
-        round_y(512, 704)
-        round_y(0, 256)
-        reduce_max(3, 15, 1)
-        round_y(256, 512)
-        turn_y(0, 5)
-        round_y(704, 832)
-        finish_on_vector(832, 1024)
-        copy_y(0, 5)
-        turn_y(1, 0)
+        copy_upper(21, 4)
+        max_to_four(20, 5, 0, 1)
+        score(2, 7, 0)
+        max_to_two(4, 4)
+        copy_upper(22, 3)
+        score(3, 0, 7)
+        max_to_four(21, 5, 1, 4)
+        copy_upper(23, 0)
+        max_to_four(22, 5, 2, 3)
+        score(3, 1, 6)
+        max_to_one(3, 4, 1, 4)
+        copy_upper(24, 7)
+        max_to_four(23, 5, 3, 0)
+        score(3, 2, 2)
+        max_to_four(24, 6, 0, 7)
+        copy_upper(25, 6)
+        add_on_vector(1, 0, 512)
+        score(3, 3, 5)
+        copy_upper(26, 2)
+        max_to_four(25, 6, 1, 6)
+        score(3, 4, 1)
+        copy_upper(27, 5)
+        max_to_four(26, 6, 2, 2)
+        max_to_two(5, 4)
+        score(3, 5, 4)
+        copy_upper(28, 1)
+        max_to_four(27, 6, 3, 5)
+        score(3, 6, 3)
+        copy_upper(29, 4)
+        max_to_one(4, 4, 2, 0)
+        max_to_one(5, 4, 2, 4)
+        score(3, 7, 0)
+        copy_upper(30, 3)
+        max_to_four(28, 7, 0, 1)
+        score(0, 8, 7)
+        max_to_four(29, 7, 1, 4)
+        copy_upper(31, 0)
+        max_to_four(30, 7, 2, 3)
+        score(0, 9, 6)
+        max_to_two(6, 4)
+        copy_upper(32, 7)
+        score(0, 10, 2)
+        max_to_four(31, 7, 3, 0)
+        copy_upper(33, 6)
+        max_to_one(6, 4, 3, 0)
+        score(0, 11, 5)
+        max_to_four(32, 8, 0, 7)
+        copy_upper(34, 2)
+        max_to_four(33, 8, 1, 6)
+        score(0, 12, 1)
+        max_to_two(7, 4)
+        copy_upper(35, 5)
+        score(0, 13, 4)
+        max_to_four(34, 8, 2, 2)
+        copy_upper(36, 1)
+        max_to_four(35, 8, 3, 5)
+        score(0, 14, 3)
+        add_on_vector(2, 0, 512)
+        copy_upper(37, 4)
+        score(0, 15, 0)
+        max_to_four(36, 9, 0, 1)
+        copy_upper(38, 3)
+        max_to_two(8, 4)
+        score(1, 8, 7)
+        copy_upper(39, 0)
+        max_to_four(37, 9, 1, 4)
+        score(1, 9, 6)
+        max_to_one(7, 4, 3, 4)
+        copy_upper(40, 7)
+        max_to_four(38, 9, 2, 3)
+        score(1, 10, 2)
+        max_to_one(8, 4, 0, 8)
+        copy_upper(41, 6)
+        max_to_four(39, 9, 3, 0)
+        score(1, 11, 5)
+        add_on_vector(3, 0, 512)
+        copy_upper(42, 2)
+        score(1, 12, 1)
+        max_to_four(40, 10, 0, 7)
+        copy_upper(43, 5)
+        max_to_four(41, 10, 1, 6)
+        score(1, 13, 4)
+        weigh(0, 512)
+        copy_upper(44, 1)
+        score(1, 14, 3)
+        max_to_four(42, 10, 2, 2)
+        round_y(0, 512)
+        max_to_two(9, 4)
+        score(1, 15, 0)
+        copy_upper(45, 4)
+        max_to_four(43, 10, 3, 5)
+        score(2, 8, 7)
+        copy_upper(46, 3)
+        max_to_four(44, 11, 0, 1)
+        copy_upper(47, 0)
+        max_to_two(10, 4)
+        score(2, 9, 6)
+        copy_upper(48, 7)
+        max_to_four(45, 11, 1, 4)
+        turn_y(0, 2)
+        max_to_four(46, 11, 2, 3)
+        copy_upper(49, 6)
+        score(2, 10, 5)
+        max_to_four(47, 11, 3, 0)
+        copy_y(0, 2)
+        max_to_four(48, 12, 0, 7)
+        max_to_one(9, 4, 0, 12)
+        score(2, 11, 1)
         quantize_y(0)
-        store_y(832, 1024)
-        store_y(512, 832)
+        copy_upper(50, 5)
+        max_to_four(49, 12, 1, 6)
+        score(2, 12, 4)
+        store_scales_of(0, 3)
+        max_to_two(11, 4)
         store_codes(0)
-        copy_y(1, 0)
+        store_y(0, 512)
+        copy_upper(51, 1)
+        store_scales_of(0, 1)
+        score(2, 13, 3)
+        max_to_four(50, 12, 2, 5)
+        copy_upper(52, 4)
+        max_to_one(11, 4, 1, 12)
+        score(2, 14, 0)
+        max_to_four(51, 12, 3, 1)
+        copy_upper(53, 3)
+        max_to_one(10, 4, 1, 8)
+        score(2, 15, 2)
+        max_to_two(12, 4)
+        copy_upper(54, 0)
+        score(3, 8, 7)
+        max_to_four(52, 13, 0, 4)
+        copy_upper(55, 2)
+        max_to_one(12, 4, 2, 8)
+        score(3, 9, 6)
+        max_to_four(53, 13, 1, 3)
+        copy_upper(56, 7)
+        max_to_four(54, 13, 2, 0)
+        store_scales_of(0, 0)
+        score(3, 10, 5)
+        max_to_four(55, 13, 3, 2)
+        copy_upper(57, 6)
+        max_to_four(56, 14, 0, 7)
+        score(3, 11, 1)
+        max_to_four(57, 14, 1, 6)
+        copy_upper(58, 5)
+        add_on_vector(1, 512, 1024)
+        score(3, 12, 4)
+        copy_upper(59, 1)
+        max_to_four(58, 14, 2, 5)
+        store_scales_of(0, 2)
+        score(3, 13, 3)
+        max_to_four(59, 14, 3, 1)
+        copy_upper(60, 4)
+        max_to_two(13, 4)
+        score(3, 14, 0)
+        copy_upper(61, 3)
+        max_to_four(60, 15, 0, 4)
+        score(3, 15, 2)
+        max_to_four(61, 15, 1, 3)
+        max_to_two(14, 4)
+        max_to_one(13, 4, 2, 12)
+        max_to_two(15, 2)
+        reduce_max(3, 14, 0)
+        add_on_vector(2, 512, 1024)
+        max_to_one(14, 4, 3, 8)
+        max_to_one(15, 2, 3, 12)
+        add_on_vector(3, 512, 768)
+        reduce_max(3, 15, 2)
+        add_on_vector(3, 768, 896)
+        weigh(512, 768)
+        weigh(768, 896)
+        add_on_vector(3, 896, 1024)
+        round_y(512, 768)
+        round_y(768, 896)
+        weigh_rounded(896, 1024)
+        weigh(896, 1024)
+        turn_y(1, 7)
+        store_y(896, 1024)
+        store_y(512, 896)
+        copy_y(1, 7)
         quantize_y(1)
         store_codes(1)
-        store_scales(2)
-        store_scales(3)
-        store_scales(0)
-        store_scales(1)
+        store_scales_of(1, 0)
+        store_scales_of(1, 1)
+        store_scales_of(1, 2)
+        store_scales_of(1, 3)

@@ -24,7 +24,10 @@ CHUNK_DOCS = BANK // DTOK
 
 FLOPS = 2 * 512 * K * (K + K + COLS)
 
-ZT = []
+ZT = [1, 2, 3]
+W_LOADS = [(0, 0, 0, 1), (0, 0, 1, 1), (0, 1, 0, 2), (1, 0, 0, 2), (1, 1, 0, 1), (1, 1, 1, 1)]
+WORD_RUNS = [(0, 2), (2, 4), (4, 8), (8, 12), (12, 16)]
+SCALE_RUNS = [(0, 8), (8, 16)]
 
 
 def tile_residual_query_maxsim_k1_kernel(
@@ -45,7 +48,7 @@ def tile_residual_query_maxsim_k1_kernel(
         warm_out = keep("warm_out", 8, F32)
         weights = (w_adapt, w_proj)
         ident16 = keep("ident16", P, BF16)
-        w_raw = [[keep("w_raw%d%d" % (w, g), 4096, BF16) for g in range(G)] for w in range(2)]
+        w_raw = {key: keep("w_raw%d%d%d" % key[:3], 2048 * key[3], BF16) for key in W_LOADS}
         w_grp = [[[keep("w_grp%d%d%d" % (w, g, h), 2048, BF16) for h in range(G)] for g in range(G)] for w in range(2)]
         w_code = [[[keep("w_code%d%d%d" % (w, g, h), 512, U32) for h in range(G)] for g in range(G)] for w in range(2)]
         w_scale = [[[keep("w_scale%d%d%d" % (w, g, h), 512, U8) for h in range(G)] for g in range(G)] for w in range(2)]
@@ -62,16 +65,16 @@ def tile_residual_query_maxsim_k1_kernel(
         h_scale = [keep("h_scale%d" % i, 256, U8) for i in range(QTOK)]
         r_code = x_code
         r_scale = x_scale
-        d_word = keep("d_word", G * 2 * COLS, U8)
-        d_scale = keep("d_scale", G * COLS, U8)
+        d_word = {c0: keep("d_word%d" % c0, G * 2 * BANK * (c1 - c0), U8) for c0, c1 in WORD_RUNS}
+        d_scale = {c0: keep("d_scale%d" % c0, G * BANK * (c1 - c0), U8) for c0, c1 in SCALE_RUNS}
         d_weight = keep("d_weight", DOCS, BF16)
         best = [keep("best%d" % i, DOCS, F32) for i in range(QTOK)]
         sum01 = keep("sum01", DOCS, F32)
         sum012 = sum01
         total = sum01
-        upper = [keep("upper%d" % n, 256, F32) for n in range(4)]
-        four = [keep("four%d" % n, 1024, F32) for n in range(2)]
-        two = [keep("two%d" % n, 512, F32) for n in range(2)]
+        upper = []
+        four = []
+        two = []
         y32 = keep("y32", DOCS, F32)
         y16 = keep("y16", DOCS, BF16)
         y_t = keep("y_t", DOCS, BF16)
@@ -88,24 +91,33 @@ def tile_residual_query_maxsim_k1_kernel(
         def bank_by_word(b):
             return banks[b][:].rearrange("p (t a) -> p a t", t=4)
 
-        def load_w(w, g, lo, hi):
+        def load_w(w, g, h, n):
             nc.sync.dma_start(
-                out=w_raw[w][g][:].rearrange("p (j c) -> p j c", j=4)[:, :, lo:hi],
-                in_=weights[w][512 * g : 512 * (g + 1), lo:hi].rearrange("(p j) c -> p j c", j=4),
+                out=w_raw[w, g, h, n][:].rearrange("p (j c) -> p j c", j=4),
+                in_=weights[w][512 * g : 512 * (g + 1), 512 * h : 512 * (h + n)].rearrange("(p j) c -> p j c", j=4),
             )
+
+        def raw_piece(w, g, h):
+            key = [k for k in W_LOADS if k[:2] == (w, g) and k[2] <= h < k[2] + k[3]][0]
+            rows = w_raw[key][:].rearrange("p (j c) -> p j c", j=4)
+            return rows[:, :, 512 * (h - key[2]) : 512 * (h - key[2] + 1)]
 
         def load_x(n):
             nc.sync.dma_start(
                 out=x_raw[n][:].rearrange("p (i k) -> p i k", i=2), in_=x[:, 2 * n : 2 * n + 2, :]
             )
 
-        d_word3 = d_word[:].rearrange("p (g n) -> p g n", g=G)
-        d_scale3 = d_scale[:].rearrange("p (g n) -> p g n", g=G)
+        def by_group(tile):
+            return tile[:].rearrange("p (g n) -> p g n", g=G)
+
+        def chunk_of(tiles, runs, width, g, c):
+            c0 = [a for a, b in runs if a <= c < b][0]
+            return by_group(tiles[c0])[:, g, width * (c - c0) : width * (c - c0 + 1)]
 
         def load_doc_words(c0, c1):
             cols = slice(2 * BANK * c0, 2 * BANK * c1)
             nc.sync.dma_start(
-                out=d_word3[:, :, cols].bitcast(I32),
+                out=by_group(d_word[c0]).bitcast(I32),
                 in_=docs_words[:, :, cols].rearrange("g p n -> p g n").bitcast(I32),
             )
 
@@ -113,34 +125,31 @@ def tile_residual_query_maxsim_k1_kernel(
             cols = slice(BANK * c0, BANK * c1)
             for r in range(4):
                 nc.sync.dma_start(
-                    out=d_scale3[r:P:32, :, cols].bitcast(I32),
+                    out=by_group(d_scale[c0])[r:P:32].bitcast(I32),
                     in_=docs_scales[:, r:16:4, cols].rearrange("g q n -> q g n").bitcast(I32),
                 )
 
         def grouped(w, g, h):
             return w_grp[w][g][h][:].rearrange("p (t m j) -> p t m j", t=4, j=4)
 
-        def weave(engine, w, g, h, m0, m1):
-            src = w_raw[w][g][:].rearrange("p (j h m t) -> p h t m j", j=4, h=G, t=4)[:, h, :, m0:m1, :]
-            dst = grouped(w, g, h)[:, :, m0:m1, :]
+        def weave(engine, w, g, h, t0, t1):
+            src = raw_piece(w, g, h).rearrange("p j (m t) -> p t m j", t=4)[:, t0:t1]
+            dst = grouped(w, g, h)[:, t0:t1]
             if engine == "V":
                 nc.vector.tensor_copy(out=dst, in_=src)
             else:
                 nc.scalar.copy(out=dst, in_=src)
 
         def weave_pe(w, g, h, e, b):
-            src = w_raw[w][g][:].rearrange("p (j c) -> p c j", j=4)
-            dst = banks[b][:].bitcast(BF16).rearrange("p (t m j) -> p m t j", t=4, j=4)
+            src = raw_piece(w, g, h).rearrange("p j (m t) -> p m t j", t=4)[:, :, 2 * e : 2 * e + 2, :]
+            dst = banks[b][:].bitcast(BF16).rearrange("p (t m j) -> p m t j", t=2, j=4)
             for s in range(2):
-                c0 = 512 * h + 256 * e + 128 * s
-                nc.tensor.matmul(
-                    out=dst[:, 32 * s : 32 * (s + 1), :, :], lhsT=ident16[:], rhs=src[:, c0 : c0 + 128, :],
-                    start=True, stop=True,
-                )
+                rows = slice(64 * s, 64 * (s + 1))
+                nc.tensor.matmul(out=dst[:, rows], lhsT=ident16[:], rhs=src[:, rows], start=True, stop=True)
 
         def weave_out(engine, w, g, h, e, b):
-            dst = grouped(w, g, h)[:, :, 64 * e : 64 * (e + 1), :]
-            src = banks[b][:].bitcast(BF16).rearrange("p (t m j) -> p t m j", t=4, j=4)
+            dst = half(w_grp[w][g][h], e)
+            src = banks[b][:].bitcast(BF16)
             if engine == "V":
                 nc.vector.tensor_copy(out=dst, in_=src)
             else:
@@ -237,8 +246,8 @@ def tile_residual_query_maxsim_k1_kernel(
                     out=banks[b][:],
                     lhsT=half(r_code[i], g).bitcast(FP8X4),
                     lhsT_scale=half(r_scale[i], g),
-                    rhs=d_word3[:, g, 2 * BANK * c : 2 * BANK * (c + 1)].bitcast(FP4X4),
-                    rhs_scale=d_scale3[:, g, BANK * c : BANK * (c + 1)],
+                    rhs=chunk_of(d_word, WORD_RUNS, 2 * BANK, g, c).bitcast(FP4X4),
+                    rhs_scale=chunk_of(d_scale, SCALE_RUNS, BANK, g, c),
                     start=(g == 0),
                     stop=(g == G - 1),
                 )
@@ -340,7 +349,8 @@ def tile_residual_query_maxsim_k1_kernel(
             make_identity(nc, ident[:])
             if with_pe:
                 make_identity(nc, ident16[:])
-            nc.vector.memset(d_scale[:].bitcast(I32), 0)
+            for c0, c1 in SCALE_RUNS:
+                nc.vector.memset(d_scale[c0][:].bitcast(I32), 0)
 
         def store_y(lo, hi):
             nc.sync.dma_start(out=out_0[:, lo:hi], in_=y32[:, lo:hi])
@@ -363,363 +373,272 @@ def tile_residual_query_maxsim_k1_kernel(
             )
 
         setup(0)
-        load_w(0, 1, 512, 1024)
-        load_w(1, 0, 0, 512)
-        load_w(0, 0, 512, 1024)
+        load_w(0, 0, 0, 1)
+        load_w(0, 0, 1, 1)
         load_x(0)
-        load_w(0, 0, 0, 512)
+        load_w(0, 1, 0, 2)
         load_x(1)
-        load_w(0, 1, 0, 512)
-        load_w(1, 1, 512, 1024)
-        load_w(1, 1, 0, 512)
-        weave("S", 0, 1, 1, 56, 128)
-        load_w(1, 0, 512, 1024)
-        weave("V", 1, 0, 0, 0, 48)
-        weave("S", 1, 0, 0, 48, 128)
+        load_w(1, 0, 0, 2)
+        load_w(1, 1, 0, 1)
+        load_w(1, 1, 1, 1)
         load_doc_scales(0, 8)
-        weave("V", 0, 0, 1, 0, 64)
-        weave("S", 0, 0, 1, 64, 128)
-        weave("V", 0, 1, 1, 0, 56)
+        weave("S", 0, 0, 0, 2, 4)
+        weave("V", 0, 0, 1, 0, 2)
+        weave("S", 0, 0, 1, 2, 4)
+        weave("V", 0, 0, 0, 0, 2)
         turn_x(1, 0)
-        quantize_w(0, 1, 1)
-        turn_x(0, 1)
         quantize_w(0, 0, 1)
+        turn_x(0, 1)
         copy_x(1, 0)
-        quantize_w(1, 0, 0)
-        weave("S", 0, 0, 0, 64, 128)
-        weave("V", 0, 0, 0, 0, 64)
-        turn_x(2, 2)
         quantize_x(1)
         copy_x(0, 1)
-        quantize_w(0, 0, 0)
-        turn_x(3, 3)
-        copy_x(2, 2)
-        load_doc_words(0, 2)
+        weave("V", 0, 1, 1, 0, 2)
+        weave("S", 0, 1, 1, 2, 4)
         quantize_x(0)
-        weave("V", 0, 1, 0, 0, 56)
-        weave("S", 0, 1, 0, 56, 128)
-        stage1(1, 1, 4)
-        quantize_x(2)
-        load_doc_words(2, 4)
-        weave("V", 1, 1, 1, 0, 72)
-        stage1(0, 1, 5)
-        copy_x(3, 3)
+        weave("V", 0, 1, 0, 0, 2)
+        load_doc_words(0, 2)
+        turn_x(3, 2)
+        weave("S", 0, 1, 0, 2, 4)
+        quantize_w(0, 1, 1)
+        stage1(0, 1, 3)
+        quantize_w(0, 0, 0)
+        copy_x(3, 2)
         quantize_w(0, 1, 0)
-        weave("S", 1, 1, 1, 72, 128)
+        load_doc_words(2, 4)
+        weave("S", 1, 0, 1, 2, 4)
+        weave("V", 1, 0, 0, 0, 2)
+        stage1(1, 1, 4)
+        h_on_vector(0, 1, 3)
         load_doc_words(4, 8)
-        stage1(0, 0, 6)
-        weave("V", 1, 1, 0, 0, 48)
-        h_on_vector(0, 1, 5)
-        stage1(2, 0, 7)
-        weave("S", 1, 1, 0, 48, 128)
-        h_on_vector(0, 0, 6)
-        load_doc_scales(8, 16)
-        stage1(2, 1, 0)
-        h_on_vector(1, 1, 4)
-        stage1(1, 0, 1)
+        weave("S", 1, 0, 0, 2, 4)
+        stage1(0, 0, 5)
         quantize_x(3)
+        weave("V", 1, 0, 1, 0, 2)
+        stage1(3, 0, 6)
+        h_on_vector(0, 0, 5)
+        load_doc_scales(8, 16)
+        weave("S", 1, 1, 1, 3, 4)
+        stage1(3, 1, 7)
+        weave("V", 1, 1, 1, 0, 3)
+        turn_x(2, 0)
         round_h(0, 1)
-        quantize_w(1, 1, 1)
-        stage1(3, 0, 2)
+        stage1(1, 0, 1)
         round_h(0, 0)
-        h_on_vector(1, 0, 1)
-        stage1(3, 1, 3)
-        weave("S", 1, 0, 1, 48, 128)
-        quantize_w(1, 1, 0)
-        load_doc_words(8, 12)
+        quantize_w(1, 0, 0)
+        copy_x(2, 0)
+        h_on_vector(1, 1, 4)
+        relu_out(3, 1, 7)
         quantize_h(0)
-        weave("V", 1, 0, 1, 0, 48)
-        stage2(0, 0, 5)
-        h_on_vector(2, 1, 0)
-        load_doc_words(12, 16)
         round_h(1, 1)
-        quantize_w(1, 0, 1)
+        quantize_x(2)
+        weave("V", 1, 1, 0, 0, 2)
+        load_doc_words(8, 12)
+        weave("S", 1, 1, 0, 2, 4)
+        stage1(2, 1, 2)
+        quantize_w(1, 1, 1)
+        stage1(2, 0, 3)
+        load_doc_words(12, 16)
+        h_on_vector(1, 0, 1)
+        h_on_pool(3, 1)
+        relu_out(2, 1, 2)
+        quantize_w(1, 1, 0)
+        stage2(0, 0, 5)
         round_h(1, 0)
-        round_h(2, 1)
         load_weight_row()
-        stage2(0, 1, 6)
+        quantize_w(1, 0, 1)
+        relu_out(2, 0, 3)
         quantize_h(1)
+        relu_out(3, 0, 6)
+        stage2(0, 1, 0)
         r_on_vector(0, 0, 5)
-        stage2(1, 0, 4)
-        r_on_vector(0, 1, 6)
-        stage2(1, 1, 1)
+        stage2(1, 1, 4)
+        h_on_pool(2, 0)
+        r_on_vector(0, 1, 0)
+        round_h(3, 1)
+        stage2(1, 0, 7)
         quantize_r_half(0, 0)
         quantize_r_half(0, 1)
-        h_on_vector(3, 1, 3)
-        score(0, 0, 0)
-        h_on_vector(2, 0, 7)
-        score(0, 1, 5)
-        copy_upper(0, 0)
-        h_on_vector(3, 0, 2)
-        score(0, 2, 6)
+        score(0, 0, 1)
+        r_on_vector(1, 0, 7)
+        score(0, 1, 2)
+        h_on_pool(2, 1)
+        reduce_max(0, 0, 1)
         round_h(2, 0)
-        max_to_four(0, 0, 0, 0)
-        score(0, 3, 3)
-        copy_upper(1, 5)
-        r_on_vector(1, 1, 1)
-        round_h(3, 0)
-        score(0, 4, 7)
-        max_to_four(1, 0, 1, 5)
-        round_h(3, 1)
+        score(0, 2, 3)
+        reduce_max(0, 1, 2)
+        score(0, 3, 6)
+        reduce_max(0, 2, 3)
+        score(0, 4, 5)
+        h_on_pool(3, 0)
+        reduce_max(0, 3, 6)
+        round_h(2, 1)
+        score(0, 5, 0)
+        r_on_vector(1, 1, 4)
+        score(0, 6, 7)
         quantize_h(2)
-        score(0, 5, 2)
-        r_on_vector(1, 0, 4)
-        copy_upper(2, 6)
-        stage2(2, 0, 0)
-        copy_upper(3, 3)
-        quantize_h(3)
-        copy_upper(4, 7)
-        max_to_four(2, 0, 2, 6)
-        score(0, 6, 1)
-        copy_upper(5, 2)
-        max_to_four(3, 0, 3, 3)
-        r_on_vector(2, 0, 0)
-        stage2(2, 1, 5)
-        copy_upper(6, 1)
+        score(0, 7, 1)
+        reduce_max(0, 4, 5)
+        round_h(3, 0)
+        stage2(2, 0, 2)
         quantize_r(1)
-        score(0, 7, 4)
-        max_to_four(4, 1, 0, 7)
-        max_to_four(5, 1, 1, 2)
-        stage2(3, 1, 6)
-        r_on_vector(2, 1, 5)
-        copy_upper(7, 4)
-        score(1, 0, 3)
-        max_to_two(0, 4)
-        score(1, 1, 0)
-        max_to_four(6, 1, 2, 1)
-        copy_upper(8, 3)
-        max_to_four(7, 1, 3, 4)
-        score(1, 2, 7)
-        quantize_r(2)
-        copy_upper(9, 0)
-        max_to_two(1, 4)
+        reduce_max(0, 5, 0)
+        stage2(2, 1, 3)
+        copy_out(2, 0, 2)
+        quantize_h(3)
+        score(1, 0, 6)
+        copy_out(2, 1, 3)
+        reduce_max(0, 6, 7)
+        r_on_pool(2, 0)
+        score(1, 1, 4)
+        reduce_max(0, 7, 1)
+        stage2(3, 1, 5)
+        reduce_max(1, 0, 6)
+        score(1, 2, 0)
+        copy_out(3, 1, 5)
+        r_on_pool(2, 1)
+        reduce_max(1, 1, 4)
         score(1, 3, 2)
-        copy_upper(10, 7)
-        max_to_four(8, 2, 0, 3)
-        score(1, 4, 5)
-        max_to_one(1, 4, 0, 4)
-        copy_upper(11, 2)
-        max_to_four(9, 2, 1, 0)
-        score(1, 5, 1)
-        max_to_four(10, 2, 2, 7)
-        copy_upper(12, 5)
-        max_to_one(0, 4, 0, 0)
-        score(1, 6, 4)
-        max_to_four(11, 2, 3, 2)
-        copy_upper(13, 1)
-        r_on_vector(3, 1, 6)
-        score(1, 7, 3)
-        copy_upper(14, 4)
-        max_to_four(12, 3, 0, 5)
-        score(2, 0, 0)
-        max_to_two(2, 4)
-        copy_upper(15, 3)
-        score(2, 1, 7)
-        max_to_four(13, 3, 1, 1)
-        copy_upper(16, 0)
-        max_to_four(14, 3, 2, 4)
-        score(2, 2, 2)
-        max_to_four(15, 3, 3, 3)
-        copy_upper(17, 7)
-        max_to_four(16, 4, 0, 0)
-        stage2(3, 0, 6)
-        max_to_four(17, 4, 1, 7)
-        copy_upper(18, 2)
-        max_to_two(3, 4)
-        score(2, 3, 5)
-        r_on_vector(3, 0, 6)
-        score(2, 4, 1)
-        copy_upper(19, 5)
-        max_to_four(18, 4, 2, 2)
-        score(2, 5, 4)
-        max_to_one(2, 4, 1, 0)
-        copy_upper(20, 1)
-        max_to_four(19, 4, 3, 5)
-        score(2, 6, 3)
-        quantize_r(3)
-        copy_upper(21, 4)
-        max_to_four(20, 5, 0, 1)
-        score(2, 7, 0)
-        max_to_two(4, 4)
-        copy_upper(22, 3)
-        score(3, 0, 7)
-        max_to_four(21, 5, 1, 4)
-        copy_upper(23, 0)
-        max_to_four(22, 5, 2, 3)
-        score(3, 1, 6)
-        max_to_one(3, 4, 1, 4)
-        copy_upper(24, 7)
-        max_to_four(23, 5, 3, 0)
-        score(3, 2, 2)
-        max_to_four(24, 6, 0, 7)
-        copy_upper(25, 6)
-        add_on_vector(1, 0, 512)
-        score(3, 3, 5)
-        copy_upper(26, 2)
-        max_to_four(25, 6, 1, 6)
-        score(3, 4, 1)
-        copy_upper(27, 5)
-        max_to_four(26, 6, 2, 2)
-        max_to_two(5, 4)
-        score(3, 5, 4)
-        copy_upper(28, 1)
-        max_to_four(27, 6, 3, 5)
-        score(3, 6, 3)
-        copy_upper(29, 4)
-        max_to_one(4, 4, 2, 0)
-        max_to_one(5, 4, 2, 4)
-        score(3, 7, 0)
-        copy_upper(30, 3)
-        max_to_four(28, 7, 0, 1)
-        score(0, 8, 7)
-        max_to_four(29, 7, 1, 4)
-        copy_upper(31, 0)
-        max_to_four(30, 7, 2, 3)
-        score(0, 9, 6)
-        max_to_two(6, 4)
-        copy_upper(32, 7)
+        reduce_max(1, 2, 0)
+        score(1, 4, 3)
+        reduce_max(1, 3, 2)
+        score(1, 5, 7)
+        r_on_pool(3, 1)
+        reduce_max(1, 4, 3)
+        score(1, 6, 1)
+        reduce_max(1, 5, 7)
+        score(1, 7, 6)
+        reduce_max(1, 6, 1)
+        score(0, 8, 5)
+        quantize_r(2)
+        score(0, 9, 4)
+        reduce_max(1, 7, 6)
+        stage2(3, 0, 0)
+        reduce_max(0, 8, 5)
         score(0, 10, 2)
-        max_to_four(31, 7, 3, 0)
-        copy_upper(33, 6)
-        max_to_one(6, 4, 3, 0)
-        score(0, 11, 5)
-        max_to_four(32, 8, 0, 7)
-        copy_upper(34, 2)
-        max_to_four(33, 8, 1, 6)
-        score(0, 12, 1)
-        max_to_two(7, 4)
-        copy_upper(35, 5)
-        score(0, 13, 4)
-        max_to_four(34, 8, 2, 2)
-        copy_upper(36, 1)
-        max_to_four(35, 8, 3, 5)
-        score(0, 14, 3)
-        add_on_vector(2, 0, 512)
-        copy_upper(37, 4)
-        score(0, 15, 0)
-        max_to_four(36, 9, 0, 1)
-        copy_upper(38, 3)
-        max_to_two(8, 4)
-        score(1, 8, 7)
-        copy_upper(39, 0)
-        max_to_four(37, 9, 1, 4)
-        score(1, 9, 6)
-        max_to_one(7, 4, 3, 4)
-        copy_upper(40, 7)
-        max_to_four(38, 9, 2, 3)
+        reduce_max(0, 9, 4)
+        copy_out(3, 0, 0)
+        score(0, 11, 3)
+        reduce_max(0, 10, 2)
+        r_on_pool(3, 0)
+        score(2, 0, 7)
+        reduce_max(0, 11, 3)
+        score(2, 1, 1)
+        reduce_max(2, 0, 7)
+        score(2, 2, 6)
+        reduce_max(2, 1, 1)
+        add_best(1, 0, 512)
+        score(2, 3, 5)
+        reduce_max(2, 2, 6)
+        score(2, 4, 4)
+        reduce_max(2, 3, 5)
+        score(2, 5, 0)
+        reduce_max(2, 4, 4)
+        score(2, 6, 2)
+        reduce_max(2, 5, 0)
+        score(2, 7, 3)
+        reduce_max(2, 6, 2)
+        score(0, 12, 7)
+        reduce_max(2, 7, 3)
+        add_best(2, 0, 512)
+        score(0, 13, 1)
+        score(0, 14, 6)
+        quantize_r(3)
+        reduce_max(0, 12, 7)
+        score(0, 15, 5)
+        reduce_max(0, 13, 1)
+        score(3, 0, 4)
+        reduce_max(0, 14, 6)
+        score(3, 1, 0)
+        reduce_max(0, 15, 5)
+        score(3, 2, 2)
+        reduce_max(3, 0, 4)
+        score(3, 3, 3)
+        reduce_max(3, 1, 0)
+        score(3, 4, 7)
+        reduce_max(3, 2, 2)
+        score(3, 5, 1)
+        score(3, 6, 6)
+        reduce_max(3, 3, 3)
+        score(3, 7, 5)
+        reduce_max(3, 4, 7)
+        score(1, 8, 4)
+        reduce_max(3, 5, 1)
+        score(1, 9, 0)
+        reduce_max(3, 6, 6)
         score(1, 10, 2)
-        max_to_one(8, 4, 0, 8)
-        copy_upper(41, 6)
-        max_to_four(39, 9, 3, 0)
-        score(1, 11, 5)
-        add_on_vector(3, 0, 512)
-        copy_upper(42, 2)
-        score(1, 12, 1)
-        max_to_four(40, 10, 0, 7)
-        copy_upper(43, 5)
-        max_to_four(41, 10, 1, 6)
-        score(1, 13, 4)
-        weigh(0, 512)
-        copy_upper(44, 1)
-        score(1, 14, 3)
-        max_to_four(42, 10, 2, 2)
-        round_y(0, 512)
-        max_to_two(9, 4)
-        score(1, 15, 0)
-        copy_upper(45, 4)
-        max_to_four(43, 10, 3, 5)
-        score(2, 8, 7)
-        copy_upper(46, 3)
-        max_to_four(44, 11, 0, 1)
-        copy_upper(47, 0)
-        max_to_two(10, 4)
-        score(2, 9, 6)
-        copy_upper(48, 7)
-        max_to_four(45, 11, 1, 4)
-        turn_y(0, 2)
-        max_to_four(46, 11, 2, 3)
-        copy_upper(49, 6)
-        score(2, 10, 5)
-        max_to_four(47, 11, 3, 0)
-        copy_y(0, 2)
-        max_to_four(48, 12, 0, 7)
-        max_to_one(9, 4, 0, 12)
-        score(2, 11, 1)
-        quantize_y(0)
-        copy_upper(50, 5)
-        max_to_four(49, 12, 1, 6)
-        score(2, 12, 4)
-        store_scales_of(0, 3)
-        max_to_two(11, 4)
-        store_codes(0)
+        reduce_max(3, 7, 5)
+        finish_on_pool(0, 512)
+        score(1, 11, 3)
+        reduce_max(1, 8, 4)
+        score(1, 12, 7)
+        reduce_max(1, 9, 0)
+        score(1, 13, 1)
+        reduce_max(1, 10, 2)
+        score(1, 14, 6)
+        reduce_max(1, 11, 3)
+        score(1, 15, 5)
+        reduce_max(1, 12, 7)
+        score(2, 8, 4)
+        reduce_max(1, 13, 1)
         store_y(0, 512)
-        copy_upper(51, 1)
-        store_scales_of(0, 1)
-        score(2, 13, 3)
-        max_to_four(50, 12, 2, 5)
-        copy_upper(52, 4)
-        max_to_one(11, 4, 1, 12)
-        score(2, 14, 0)
-        max_to_four(51, 12, 3, 1)
-        copy_upper(53, 3)
-        max_to_one(10, 4, 1, 8)
-        score(2, 15, 2)
-        max_to_two(12, 4)
-        copy_upper(54, 0)
-        score(3, 8, 7)
-        max_to_four(52, 13, 0, 4)
-        copy_upper(55, 2)
-        max_to_one(12, 4, 2, 8)
-        score(3, 9, 6)
-        max_to_four(53, 13, 1, 3)
-        copy_upper(56, 7)
-        max_to_four(54, 13, 2, 0)
+        round_y(0, 512)
+        score(2, 9, 0)
+        reduce_max(1, 14, 6)
+        score(2, 10, 2)
+        reduce_max(1, 15, 5)
+        add_best(1, 512, 1024)
+        score(2, 11, 3)
+        reduce_max(2, 8, 4)
+        score(2, 12, 7)
+        reduce_max(2, 9, 0)
+        score(2, 13, 1)
+        reduce_max(2, 10, 2)
+        score(2, 14, 6)
+        reduce_max(2, 11, 3)
+        score(2, 15, 5)
+        reduce_max(2, 12, 7)
+        score(3, 8, 4)
+        score(3, 9, 0)
+        reduce_max(2, 13, 1)
+        score(3, 10, 2)
+        reduce_max(2, 14, 6)
+        score(3, 11, 3)
+        reduce_max(2, 15, 5)
+        add_best(2, 512, 1024)
+        score(3, 12, 7)
+        reduce_max(3, 8, 4)
+        score(3, 13, 1)
+        reduce_max(3, 9, 0)
+        score(3, 14, 6)
+        reduce_max(3, 10, 2)
+        score(3, 15, 5)
+        reduce_max(3, 11, 3)
+        finish_on_pool(512, 704)
+        turn_y(0, 4)
+        reduce_max(3, 12, 7)
+        copy_y(0, 4)
+        reduce_max(3, 13, 1)
+        reduce_max(3, 14, 6)
+        finish_on_pool(704, 832)
+        round_y(512, 704)
+        quantize_y(0)
+        reduce_max(3, 15, 5)
+        store_codes(0)
         store_scales_of(0, 0)
-        score(3, 10, 5)
-        max_to_four(55, 13, 3, 2)
-        copy_upper(57, 6)
-        max_to_four(56, 14, 0, 7)
-        score(3, 11, 1)
-        max_to_four(57, 14, 1, 6)
-        copy_upper(58, 5)
-        add_on_vector(1, 512, 1024)
-        score(3, 12, 4)
-        copy_upper(59, 1)
-        max_to_four(58, 14, 2, 5)
+        store_scales_of(0, 1)
+        store_scales_of(0, 3)
+        add_on_vector(3, 832, 1024)
+        round_y(704, 832)
         store_scales_of(0, 2)
-        score(3, 13, 3)
-        max_to_four(59, 14, 3, 1)
-        copy_upper(60, 4)
-        max_to_two(13, 4)
-        score(3, 14, 0)
-        copy_upper(61, 3)
-        max_to_four(60, 15, 0, 4)
-        score(3, 15, 2)
-        max_to_four(61, 15, 1, 3)
-        max_to_two(14, 4)
-        max_to_one(13, 4, 2, 12)
-        max_to_two(15, 2)
-        reduce_max(3, 14, 0)
-        add_on_vector(2, 512, 1024)
-        max_to_one(14, 4, 3, 8)
-        max_to_one(15, 2, 3, 12)
-        add_on_vector(3, 512, 768)
-        reduce_max(3, 15, 2)
-        add_on_vector(3, 768, 896)
-        weigh(512, 768)
-        weigh(768, 896)
-        add_on_vector(3, 896, 1024)
-        round_y(512, 768)
-        round_y(768, 896)
-        weigh_rounded(896, 1024)
-        weigh(896, 1024)
-        turn_y(1, 7)
-        store_y(896, 1024)
-        store_y(512, 896)
-        copy_y(1, 7)
+        weigh_rounded(832, 1024)
+        weigh(832, 1024)
+        turn_y(1, 0)
+        store_y(832, 1024)
+        store_y(512, 832)
+        copy_y(1, 0)
         quantize_y(1)
         store_codes(1)
-        store_scales_of(1, 0)
-        store_scales_of(1, 1)
         store_scales_of(1, 2)
         store_scales_of(1, 3)
+        store_scales_of(1, 0)
+        store_scales_of(1, 1)

@@ -24,9 +24,9 @@ CHUNK_DOCS = BANK // DTOK
 
 FLOPS = 2 * 512 * K * (K + K + COLS)
 
-ZT = [1, 2, 3]
+ZT = [2, 3]
 W_LOADS = [(0, 0, 0, 1), (0, 0, 1, 1), (0, 1, 0, 2), (1, 0, 0, 2), (1, 1, 0, 1), (1, 1, 1, 1)]
-WORD_RUNS = [(0, 2), (2, 4), (4, 8), (8, 12), (12, 16)]
+WORD_RUNS = [(0, 2), (2, 4), (4, 6), (6, 8), (8, 12), (12, 16)]
 SCALE_RUNS = [(0, 8), (8, 16)]
 
 
@@ -49,7 +49,7 @@ def tile_residual_query_maxsim_k1_kernel(
         weights = (w_adapt, w_proj)
         ident16 = keep("ident16", P, BF16)
         w_raw = {key: keep("w_raw%d%d%d" % key[:3], 2048 * key[3], BF16) for key in W_LOADS}
-        w_grp = [[[keep("w_grp%d%d%d" % (w, g, h), 2048, BF16) for h in range(G)] for g in range(G)] for w in range(2)]
+        w_grp = [[[keep("w_grp%d%d" % (g, h), 2048, BF16) for h in range(G)] for g in range(G)]] * 2
         w_code = [[[keep("w_code%d%d%d" % (w, g, h), 512, U32) for h in range(G)] for g in range(G)] for w in range(2)]
         w_scale = [[[keep("w_scale%d%d%d" % (w, g, h), 512, U8) for h in range(G)] for g in range(G)] for w in range(2)]
         x_raw = [keep("x_raw%d" % n, 2 * K, BF16) for n in range(2)]
@@ -288,6 +288,13 @@ def tile_residual_query_maxsim_k1_kernel(
                 in0=src[:, :, 0], in1=src[:, :, 1], op=ALU.max,
             )
 
+        def add_on_pool(i, lo, hi):
+            first = best[0] if i == 1 else sum01
+            nc.gpsimd.tensor_tensor(out=sum01[:, lo:hi], in0=first[:, lo:hi], in1=best[i][:, lo:hi], op=ALU.add)
+
+        def weigh_on_pool(lo, hi):
+            nc.gpsimd.tensor_tensor(out=y32[:, lo:hi], in0=sum01[:, lo:hi], in1=d_weight[:, lo:hi], op=ALU.mult)
+
         def add_on_vector(i, lo, hi):
             first = best[0] if i == 1 else sum01
             nc.vector.tensor_tensor(out=sum01[:, lo:hi], in0=first[:, lo:hi], in1=best[i][:, lo:hi], op=ALU.add)
@@ -372,273 +379,283 @@ def tile_residual_query_maxsim_k1_kernel(
                 out=out_1[g].rearrange("p m t -> p (m t)").bitcast(I32), in_=half(y_code, g).bitcast(I32)
             )
 
-        setup(0)
-        load_w(0, 0, 0, 1)
-        load_w(0, 0, 1, 1)
+        setup(1)
         load_x(0)
-        load_w(0, 1, 0, 2)
+        load_w(0, 0, 0, 1)
         load_x(1)
+        load_w(0, 0, 1, 1)
+        load_w(0, 1, 0, 2)
         load_w(1, 0, 0, 2)
         load_w(1, 1, 0, 1)
         load_w(1, 1, 1, 1)
         load_doc_scales(0, 8)
+        turn_x(0, 0)
+        turn_x(1, 1)
         weave("S", 0, 0, 0, 2, 4)
-        weave("V", 0, 0, 1, 0, 2)
-        weave("S", 0, 0, 1, 2, 4)
         weave("V", 0, 0, 0, 0, 2)
-        turn_x(1, 0)
-        quantize_w(0, 0, 1)
-        turn_x(0, 1)
-        copy_x(1, 0)
-        quantize_x(1)
-        copy_x(0, 1)
-        weave("V", 0, 1, 1, 0, 2)
-        weave("S", 0, 1, 1, 2, 4)
-        quantize_x(0)
-        weave("V", 0, 1, 0, 0, 2)
-        load_doc_words(0, 2)
-        turn_x(3, 2)
-        weave("S", 0, 1, 0, 2, 4)
-        quantize_w(0, 1, 1)
-        stage1(0, 1, 3)
+        turn_x(2, 2)
+        copy_x(0, 0)
         quantize_w(0, 0, 0)
-        copy_x(3, 2)
+        turn_x(3, 3)
+        copy_x(1, 1)
+        weave("V", 0, 0, 1, 0, 2)
+        weave_pe(0, 0, 1, 1, 4)
+        copy_x(2, 2)
+        copy_x(3, 3)
+        quantize_x(0)
+        quantize_x(1)
+        quantize_x(2)
+        quantize_x(3)
+        weave_out("S", 0, 0, 1, 1, 4)
+        load_doc_words(0, 2)
+        weave("V", 0, 1, 0, 0, 2)
+        weave_pe(0, 1, 1, 1, 5)
+        weave("S", 0, 1, 0, 2, 4)
+        quantize_w(0, 0, 1)
+        weave("V", 0, 1, 1, 0, 2)
+        weave_out("S", 0, 1, 1, 1, 5)
         quantize_w(0, 1, 0)
         load_doc_words(2, 4)
-        weave("S", 1, 0, 1, 2, 4)
+        weave_pe(1, 0, 0, 1, 6)
+        weave("S", 1, 0, 1, 0, 2)
+        quantize_w(0, 1, 1)
+        stage1(0, 0, 7)
         weave("V", 1, 0, 0, 0, 2)
-        stage1(1, 1, 4)
-        h_on_vector(0, 1, 3)
-        load_doc_words(4, 8)
-        weave("S", 1, 0, 0, 2, 4)
-        stage1(0, 0, 5)
-        quantize_x(3)
-        weave("V", 1, 0, 1, 0, 2)
-        stage1(3, 0, 6)
-        h_on_vector(0, 0, 5)
-        load_doc_scales(8, 16)
-        weave("S", 1, 1, 1, 3, 4)
-        stage1(3, 1, 7)
-        weave("V", 1, 1, 1, 0, 3)
-        turn_x(2, 0)
-        round_h(0, 1)
-        stage1(1, 0, 1)
+        stage1(0, 1, 0)
+        load_doc_words(4, 6)
+        weave_out("S", 1, 0, 0, 1, 6)
+        h_on_vector(0, 0, 7)
+        weave_pe(1, 1, 0, 1, 1)
+        h_on_vector(0, 1, 0)
         round_h(0, 0)
+        stage1(1, 1, 2)
+        load_doc_words(6, 8)
         quantize_w(1, 0, 0)
-        copy_x(2, 0)
-        h_on_vector(1, 1, 4)
-        relu_out(3, 1, 7)
-        quantize_h(0)
-        round_h(1, 1)
-        quantize_x(2)
+        round_h(0, 1)
+        weave_pe(1, 0, 1, 1, 3)
         weave("V", 1, 1, 0, 0, 2)
-        load_doc_words(8, 12)
-        weave("S", 1, 1, 0, 2, 4)
-        stage1(2, 1, 2)
-        quantize_w(1, 1, 1)
-        stage1(2, 0, 3)
-        load_doc_words(12, 16)
-        h_on_vector(1, 0, 1)
-        h_on_pool(3, 1)
-        relu_out(2, 1, 2)
+        load_doc_scales(8, 16)
+        weave_out("S", 1, 1, 0, 1, 1)
+        weave_pe(1, 1, 1, 1, 4)
+        quantize_h(0)
+        weave("V", 1, 1, 1, 0, 2)
+        stage1(3, 0, 5)
+        weave_out("S", 1, 1, 1, 1, 4)
         quantize_w(1, 1, 0)
-        stage2(0, 0, 5)
-        round_h(1, 0)
-        load_weight_row()
+        stage1(2, 1, 6)
+        weave_out("S", 1, 0, 1, 1, 3)
+        quantize_w(1, 1, 1)
+        stage1(2, 0, 7)
+        relu_out(2, 1, 6)
         quantize_w(1, 0, 1)
-        relu_out(2, 0, 3)
-        quantize_h(1)
-        relu_out(3, 0, 6)
-        stage2(0, 1, 0)
-        r_on_vector(0, 0, 5)
-        stage2(1, 1, 4)
-        h_on_pool(2, 0)
-        r_on_vector(0, 1, 0)
-        round_h(3, 1)
-        stage2(1, 0, 7)
+        stage2(0, 0, 0)
+        h_on_vector(1, 1, 2)
+        h_on_pool(2, 1)
+        stage2(0, 1, 1)
+        load_doc_words(8, 12)
+        r_on_vector(0, 0, 0)
+        round_h(1, 1)
+        stage1(1, 0, 4)
+        r_on_vector(0, 1, 1)
+        relu_out(2, 0, 7)
+        stage1(3, 1, 3)
+        load_doc_words(12, 16)
         quantize_r_half(0, 0)
         quantize_r_half(0, 1)
-        score(0, 0, 1)
-        r_on_vector(1, 0, 7)
-        score(0, 1, 2)
-        h_on_pool(2, 1)
-        reduce_max(0, 0, 1)
-        round_h(2, 0)
-        score(0, 2, 3)
-        reduce_max(0, 1, 2)
-        score(0, 3, 6)
-        reduce_max(0, 2, 3)
-        score(0, 4, 5)
-        h_on_pool(3, 0)
-        reduce_max(0, 3, 6)
         round_h(2, 1)
-        score(0, 5, 0)
-        r_on_vector(1, 1, 4)
-        score(0, 6, 7)
+        h_on_vector(1, 0, 4)
+        score(0, 0, 6)
+        h_on_pool(2, 0)
+        score(0, 1, 2)
+        round_h(1, 0)
+        reduce_max(0, 0, 6)
+        load_weight_row()
+        score(0, 2, 0)
+        relu_out(3, 1, 3)
+        reduce_max(0, 1, 2)
+        score(0, 3, 1)
+        round_h(2, 0)
+        quantize_h(1)
+        score(0, 4, 7)
+        reduce_max(0, 2, 0)
+        h_on_pool(3, 1)
+        relu_out(3, 0, 5)
+        stage2(1, 1, 4)
         quantize_h(2)
-        score(0, 7, 1)
-        reduce_max(0, 4, 5)
-        round_h(3, 0)
-        stage2(2, 0, 2)
+        reduce_max(0, 3, 1)
+        stage2(1, 0, 6)
+        reduce_max(0, 4, 7)
+        score(0, 5, 3)
+        h_on_pool(3, 0)
+        round_h(3, 1)
+        r_on_vector(1, 0, 6)
+        stage2(2, 1, 2)
+        r_on_vector(1, 1, 4)
+        stage2(2, 0, 0)
         quantize_r(1)
-        reduce_max(0, 5, 0)
-        stage2(2, 1, 3)
-        copy_out(2, 0, 2)
+        score(0, 6, 5)
+        round_h(3, 0)
+        reduce_max(0, 5, 3)
+        score(0, 7, 1)
+        copy_out(2, 0, 0)
         quantize_h(3)
-        score(1, 0, 6)
-        copy_out(2, 1, 3)
-        reduce_max(0, 6, 7)
-        r_on_pool(2, 0)
-        score(1, 1, 4)
+        score(1, 0, 7)
+        reduce_max(0, 6, 5)
+        copy_out(2, 1, 2)
+        score(1, 1, 6)
         reduce_max(0, 7, 1)
-        stage2(3, 1, 5)
-        reduce_max(1, 0, 6)
-        score(1, 2, 0)
-        copy_out(3, 1, 5)
         r_on_pool(2, 1)
-        reduce_max(1, 1, 4)
-        score(1, 3, 2)
-        reduce_max(1, 2, 0)
-        score(1, 4, 3)
-        reduce_max(1, 3, 2)
-        score(1, 5, 7)
-        r_on_pool(3, 1)
-        reduce_max(1, 4, 3)
-        score(1, 6, 1)
-        reduce_max(1, 5, 7)
-        score(1, 7, 6)
-        reduce_max(1, 6, 1)
-        score(0, 8, 5)
-        quantize_r(2)
-        score(0, 9, 4)
-        reduce_max(1, 7, 6)
+        score(1, 2, 4)
+        reduce_max(1, 0, 7)
+        score(1, 3, 3)
+        reduce_max(1, 1, 6)
         stage2(3, 0, 0)
-        reduce_max(0, 8, 5)
-        score(0, 10, 2)
-        reduce_max(0, 9, 4)
+        reduce_max(1, 2, 4)
+        r_on_pool(2, 0)
+        score(1, 4, 5)
+        reduce_max(1, 3, 3)
         copy_out(3, 0, 0)
-        score(0, 11, 3)
-        reduce_max(0, 10, 2)
+        score(1, 5, 2)
+        reduce_max(1, 4, 5)
         r_on_pool(3, 0)
-        score(2, 0, 7)
-        reduce_max(0, 11, 3)
-        score(2, 1, 1)
-        reduce_max(2, 0, 7)
-        score(2, 2, 6)
-        reduce_max(2, 1, 1)
-        add_best(1, 0, 512)
-        score(2, 3, 5)
-        reduce_max(2, 2, 6)
+        score(1, 6, 1)
+        reduce_max(1, 5, 2)
+        score(1, 7, 7)
+        reduce_max(1, 6, 1)
+        score(0, 8, 6)
+        reduce_max(1, 7, 7)
+        score(0, 9, 4)
+        quantize_r(2)
+        score(0, 10, 3)
+        reduce_max(0, 8, 6)
+        add_on_pool(1, 0, 512)
+        score(0, 11, 0)
+        reduce_max(0, 9, 4)
+        score(2, 0, 5)
+        reduce_max(0, 10, 3)
+        score(2, 1, 2)
+        reduce_max(0, 11, 0)
+        score(2, 2, 1)
+        reduce_max(2, 0, 5)
+        score(2, 3, 7)
+        reduce_max(2, 1, 2)
+        stage2(3, 1, 6)
+        reduce_max(2, 2, 1)
         score(2, 4, 4)
-        reduce_max(2, 3, 5)
-        score(2, 5, 0)
+        reduce_max(2, 3, 7)
+        copy_out(3, 1, 6)
+        score(2, 5, 3)
         reduce_max(2, 4, 4)
-        score(2, 6, 2)
-        reduce_max(2, 5, 0)
-        score(2, 7, 3)
-        reduce_max(2, 6, 2)
-        score(0, 12, 7)
-        reduce_max(2, 7, 3)
-        add_best(2, 0, 512)
+        r_on_pool(3, 1)
+        score(2, 6, 0)
+        reduce_max(2, 5, 3)
+        score(2, 7, 5)
+        reduce_max(2, 6, 0)
+        score(0, 12, 2)
+        reduce_max(2, 7, 5)
         score(0, 13, 1)
-        score(0, 14, 6)
         quantize_r(3)
-        reduce_max(0, 12, 7)
-        score(0, 15, 5)
+        score(0, 14, 7)
+        reduce_max(0, 12, 2)
+        add_on_pool(2, 0, 512)
+        score(0, 15, 6)
         reduce_max(0, 13, 1)
         score(3, 0, 4)
-        reduce_max(0, 14, 6)
-        score(3, 1, 0)
-        reduce_max(0, 15, 5)
-        score(3, 2, 2)
+        reduce_max(0, 14, 7)
+        score(3, 1, 3)
+        reduce_max(0, 15, 6)
+        score(3, 2, 0)
         reduce_max(3, 0, 4)
-        score(3, 3, 3)
-        reduce_max(3, 1, 0)
-        score(3, 4, 7)
-        reduce_max(3, 2, 2)
+        score(3, 3, 5)
+        reduce_max(3, 1, 3)
+        score(3, 4, 2)
+        reduce_max(3, 2, 0)
         score(3, 5, 1)
-        score(3, 6, 6)
-        reduce_max(3, 3, 3)
-        score(3, 7, 5)
-        reduce_max(3, 4, 7)
-        score(1, 8, 4)
+        reduce_max(3, 3, 5)
+        score(3, 6, 7)
+        reduce_max(3, 4, 2)
+        score(3, 7, 6)
         reduce_max(3, 5, 1)
-        score(1, 9, 0)
-        reduce_max(3, 6, 6)
-        score(1, 10, 2)
-        reduce_max(3, 7, 5)
-        finish_on_pool(0, 512)
-        score(1, 11, 3)
+        score(1, 8, 4)
+        reduce_max(3, 6, 7)
+        score(1, 9, 3)
+        reduce_max(3, 7, 6)
+        score(1, 10, 0)
         reduce_max(1, 8, 4)
-        score(1, 12, 7)
-        reduce_max(1, 9, 0)
+        add_on_pool(3, 0, 512)
+        score(1, 11, 5)
+        reduce_max(1, 9, 3)
+        score(1, 12, 2)
+        reduce_max(1, 10, 0)
         score(1, 13, 1)
-        reduce_max(1, 10, 2)
-        score(1, 14, 6)
-        reduce_max(1, 11, 3)
-        score(1, 15, 5)
-        reduce_max(1, 12, 7)
-        score(2, 8, 4)
+        reduce_max(1, 11, 5)
+        weigh_on_pool(0, 512)
+        score(1, 14, 7)
+        reduce_max(1, 12, 2)
+        score(1, 15, 6)
         reduce_max(1, 13, 1)
+        score(2, 8, 4)
+        reduce_max(1, 14, 7)
         store_y(0, 512)
         round_y(0, 512)
-        score(2, 9, 0)
-        reduce_max(1, 14, 6)
-        score(2, 10, 2)
-        reduce_max(1, 15, 5)
-        add_best(1, 512, 1024)
-        score(2, 11, 3)
+        score(2, 9, 3)
+        reduce_max(1, 15, 6)
+        score(2, 10, 0)
         reduce_max(2, 8, 4)
-        score(2, 12, 7)
-        reduce_max(2, 9, 0)
-        score(2, 13, 1)
-        reduce_max(2, 10, 2)
+        add_on_pool(1, 512, 1024)
+        score(2, 11, 5)
+        reduce_max(2, 9, 3)
+        score(2, 12, 2)
+        reduce_max(2, 10, 0)
+        turn_y(0, 1)
+        reduce_max(2, 11, 5)
+        score(2, 13, 7)
+        copy_y(0, 1)
+        reduce_max(2, 12, 2)
         score(2, 14, 6)
-        reduce_max(2, 11, 3)
-        score(2, 15, 5)
-        reduce_max(2, 12, 7)
-        score(3, 8, 4)
-        score(3, 9, 0)
-        reduce_max(2, 13, 1)
-        score(3, 10, 2)
+        reduce_max(2, 13, 7)
+        score(2, 15, 4)
         reduce_max(2, 14, 6)
-        score(3, 11, 3)
-        reduce_max(2, 15, 5)
-        add_best(2, 512, 1024)
-        score(3, 12, 7)
-        reduce_max(3, 8, 4)
-        score(3, 13, 1)
+        score(3, 8, 3)
+        reduce_max(2, 15, 4)
+        score(3, 9, 0)
+        reduce_max(3, 8, 3)
+        add_on_pool(2, 512, 1024)
+        score(3, 10, 5)
         reduce_max(3, 9, 0)
+        score(3, 11, 1)
+        reduce_max(3, 10, 5)
+        score(3, 12, 2)
+        reduce_max(3, 11, 1)
+        score(3, 13, 7)
+        add_on_pool(3, 512, 704)
+        reduce_max(3, 12, 2)
         score(3, 14, 6)
-        reduce_max(3, 10, 2)
-        score(3, 15, 5)
-        reduce_max(3, 11, 3)
-        finish_on_pool(512, 704)
-        turn_y(0, 4)
-        reduce_max(3, 12, 7)
-        copy_y(0, 4)
-        reduce_max(3, 13, 1)
+        reduce_max(3, 13, 7)
+        score(3, 15, 4)
+        add_on_pool(3, 704, 832)
         reduce_max(3, 14, 6)
-        finish_on_pool(704, 832)
+        weigh_on_pool(512, 704)
+        reduce_max(3, 15, 4)
+        weigh_on_pool(704, 832)
         round_y(512, 704)
         quantize_y(0)
-        reduce_max(3, 15, 5)
+        add_on_vector(3, 832, 1024)
+        store_scales_of(0, 3)
+        store_scales_of(0, 2)
         store_codes(0)
         store_scales_of(0, 0)
         store_scales_of(0, 1)
-        store_scales_of(0, 3)
-        add_on_vector(3, 832, 1024)
         round_y(704, 832)
-        store_scales_of(0, 2)
         weigh_rounded(832, 1024)
-        weigh(832, 1024)
-        turn_y(1, 0)
-        store_y(832, 1024)
         store_y(512, 832)
-        copy_y(1, 0)
+        weigh(832, 1024)
+        turn_y(1, 3)
+        store_y(832, 1024)
+        copy_y(1, 3)
         quantize_y(1)
         store_codes(1)
-        store_scales_of(1, 2)
-        store_scales_of(1, 3)
         store_scales_of(1, 0)
         store_scales_of(1, 1)
+        store_scales_of(1, 2)
+        store_scales_of(1, 3)

@@ -12,28 +12,37 @@ FP8X4 = mybir.dt.float8_e4m3fn_x4
 FP4X4 = mybir.dt.float4_e2m1fn_x4
 ALU = mybir.AluOpType
 ACT = mybir.ActivationFunctionType
-AXIS_X = mybir.AxisListType.X
 
 P = 128
 QTOK, DOCS, DTOK, K = 4, 1024, 8, 1024
-COLS = DOCS * DTOK
-G = K // 512
+GROUP = 512
+G = K // GROUP
 BANK = 512
-CHUNKS = COLS // BANK
+BANKS = 8
 CHUNK_DOCS = BANK // DTOK
+CHUNKS = DOCS // CHUNK_DOCS
+HALF_CHUNKS = CHUNKS // 2
+ADAPT, PROJ = 0, 1
 
-FLOPS = 2 * 512 * K * (K + K + COLS)
+FLOPS = 2 * P * QTOK * K * (K + K + DOCS * DTOK)
 
-ZT = [2, 3]
-W_LOADS = [(0, 0, 0, 1), (0, 0, 1, 1), (0, 1, 0, 2), (1, 0, 0, 2), (1, 1, 0, 1), (1, 1, 1, 1)]
-WORD_RUNS = [(0, 2), (2, 4), (4, 6), (6, 8), (8, 12), (12, 16)]
-SCALE_RUNS = [(0, 8), (8, 16)]
+WEIGHT_LOADS = [(ADAPT, 0, 0, 2), (ADAPT, 1, 0, 2), (PROJ, 0, 0, 2), (PROJ, 1, 0, 1), (PROJ, 1, 1, 1)]
+WORD_LOADS = [(0, 2), (2, 4), (4, 6), (6, 8), (8, 12), (12, 16)]
+SCALE_LOADS = [(0, HALF_CHUNKS), (HALF_CHUNKS, CHUNKS)]
+
+SWEEPS = [(0, 0), (1, 0), (2, 0), (0, 1), (1, 1), (3, 0), (2, 1), (3, 1)]
+JOBS = [(i, HALF_CHUNKS * s + c) for i, s in SWEEPS for c in range(HALF_CHUNKS)]
+
+POOL_TILES = (2, 3)
+POOL_PIECE = 256
+POOL_END = 704
 
 
 def tile_residual_query_maxsim_k1_kernel(
     tc, x, w_adapt, w_proj, docs_words, docs_scales, doc_weight, out_0, out_1, out_2
 ):
     nc = tc.nc
+    weights = (w_adapt, w_proj)
     with ExitStack() as ctx:
         sb = ctx.enter_context(tc.tile_pool(name="sb", bufs=1))
         ps = ctx.enter_context(tc.psum_pool(name="ps", bufs=1))
@@ -42,82 +51,79 @@ def tile_residual_query_maxsim_k1_kernel(
         def keep(name, width, dtype):
             return sb.tile([P, width], dtype, name=name, align_bytes=64)
 
-        banks = [ps.tile([P, BANK], F32, name="bank%d" % b) for b in range(8)]
-        ident = keep("ident", P, F32)
-        warm_in = keep("warm_in", 8, F32)
-        warm_out = keep("warm_out", 8, F32)
-        weights = (w_adapt, w_proj)
+        def per_tile(name, width, dtype, tiles):
+            return {i: keep("%s%d" % (name, i), width, dtype) for i in tiles}
+
+        pieces = [(w, g, h) for w in (ADAPT, PROJ) for g in range(G) for h in range(G)]
+        banks = [ps.tile([P, BANK], F32, name="bank%d" % b) for b in range(BANKS)]
+        ident32 = keep("ident32", P, F32)
         ident16 = keep("ident16", P, BF16)
-        w_raw = {key: keep("w_raw%d%d%d" % key[:3], 2048 * key[3], BF16) for key in W_LOADS}
-        w_grp = [[[keep("w_grp%d%d" % (g, h), 2048, BF16) for h in range(G)] for g in range(G)]] * 2
-        w_code = [[[keep("w_code%d%d%d" % (w, g, h), 512, U32) for h in range(G)] for g in range(G)] for w in range(2)]
-        w_scale = [[[keep("w_scale%d%d%d" % (w, g, h), 512, U8) for h in range(G)] for g in range(G)] for w in range(2)]
-        x_raw = [keep("x_raw%d" % n, 2 * K, BF16) for n in range(2)]
-        x_t = [keep("x_t%d" % i, K, BF16) for i in range(QTOK)]
-        z1 = {i: keep("z_%d" % i, K, F32) for i in ZT}
-        z2 = z1
-        h32 = [keep("h32_%d" % i, K, F32) for i in range(QTOK)]
-        h16 = [keep("h16_%d" % i, K, BF16) for i in range(QTOK)]
-        r16 = h16
-        x_code = [keep("x_code%d" % i, 256, U32) for i in range(QTOK)]
-        x_scale = [keep("x_scale%d" % i, 256, U8) for i in range(QTOK)]
-        h_code = [keep("h_code%d" % i, 256, U32) for i in range(QTOK)]
-        h_scale = [keep("h_scale%d" % i, 256, U8) for i in range(QTOK)]
-        r_code = x_code
-        r_scale = x_scale
-        d_word = {c0: keep("d_word%d" % c0, G * 2 * BANK * (c1 - c0), U8) for c0, c1 in WORD_RUNS}
-        d_scale = {c0: keep("d_scale%d" % c0, G * BANK * (c1 - c0), U8) for c0, c1 in SCALE_RUNS}
-        d_weight = keep("d_weight", DOCS, BF16)
-        best = [keep("best%d" % i, DOCS, F32) for i in range(QTOK)]
-        sum01 = keep("sum01", DOCS, F32)
-        sum012 = sum01
-        total = sum01
-        upper = []
-        four = []
-        two = []
+        w_rows = {load: keep("w_rows%d%d%d" % load[:3], 4 * GROUP * load[3], BF16) for load in WEIGHT_LOADS}
+        w_words = {(g, h): keep("w_words%d%d" % (g, h), 4 * GROUP, BF16) for g in range(G) for h in range(G)}
+        w_code = {piece: keep("w_code%d%d%d" % piece, GROUP, U32) for piece in pieces}
+        w_scale = {piece: keep("w_scale%d%d%d" % piece, GROUP, U8) for piece in pieces}
+        x_rows = per_tile("x_rows", 2 * K, BF16, range(QTOK // 2))
+        x16 = per_tile("x16_", K, BF16, range(QTOK))
+        h32 = per_tile("h32_", K, F32, range(QTOK))
+        h16 = per_tile("h16_", K, BF16, range(QTOK))
+        r16 = per_tile("r16_", K, BF16, range(QTOK))
+        relu32 = per_tile("relu32_", K, F32, POOL_TILES)
+        proj32 = per_tile("proj32_", K, F32, POOL_TILES)
+        x_code = per_tile("x_code", G * P, U32, range(QTOK))
+        x_scale = per_tile("x_scale", G * P, U8, range(QTOK))
+        h_code = per_tile("h_code", G * P, U32, range(QTOK))
+        h_scale = per_tile("h_scale", G * P, U8, range(QTOK))
+        r_code = per_tile("r_code", G * P, U32, range(QTOK))
+        r_scale = per_tile("r_scale", G * P, U8, range(QTOK))
+        doc_code = {c0: keep("doc_code%d" % c0, G * 2 * BANK * (c1 - c0), U8) for c0, c1 in WORD_LOADS}
+        doc_scale = {c0: keep("doc_scale%d" % c0, G * BANK * (c1 - c0), U8) for c0, c1 in SCALE_LOADS}
+        doc_gain = keep("doc_gain", DOCS, BF16)
+        best = per_tile("best", DOCS, F32, range(QTOK))
+        total = keep("total", DOCS, F32)
         y32 = keep("y32", DOCS, F32)
         y16 = keep("y16", DOCS, BF16)
-        y_t = keep("y_t", DOCS, BF16)
-        y_code = keep("y_code", 256, U32)
-        y_scale = keep("y_scale", 256, U8)
+        y_words = keep("y_words", DOCS, BF16)
+        y_code = keep("y_code", G * P, U32)
+        y_scale = keep("y_scale", G * P, U8)
 
-        def half(tile, h):
-            n = tile.shape[1] // 2
-            return tile[:, h * n : (h + 1) * n]
-
-        def by_word(ap):
-            return ap.rearrange("p (a t) -> p a t", t=4)
-
-        def bank_by_word(b):
-            return banks[b][:].rearrange("p (t a) -> p a t", t=4)
-
-        def load_w(w, g, h, n):
-            nc.sync.dma_start(
-                out=w_raw[w, g, h, n][:].rearrange("p (j c) -> p j c", j=4),
-                in_=weights[w][512 * g : 512 * (g + 1), 512 * h : 512 * (h + n)].rearrange("(p j) c -> p j c", j=4),
-            )
-
-        def raw_piece(w, g, h):
-            key = [k for k in W_LOADS if k[:2] == (w, g) and k[2] <= h < k[2] + k[3]][0]
-            rows = w_raw[key][:].rearrange("p (j c) -> p j c", j=4)
-            return rows[:, :, 512 * (h - key[2]) : 512 * (h - key[2] + 1)]
-
-        def load_x(n):
-            nc.sync.dma_start(
-                out=x_raw[n][:].rearrange("p (i k) -> p i k", i=2), in_=x[:, 2 * n : 2 * n + 2, :]
-            )
+        def half(tile, n):
+            width = tile.shape[1] // 2
+            return tile[:, n * width : (n + 1) * width]
 
         def by_group(tile):
             return tile[:].rearrange("p (g n) -> p g n", g=G)
 
-        def chunk_of(tiles, runs, width, g, c):
-            c0 = [a for a, b in runs if a <= c < b][0]
-            return by_group(tiles[c0])[:, g, width * (c - c0) : width * (c - c0 + 1)]
+        def by_word(ap):
+            return ap.rearrange("p (a t) -> p a t", t=4)
+
+        free_banks = list(range(BANKS))
+        holder = {}
+
+        def take_bank(result):
+            holder[result] = free_banks.pop(0)
+            return banks[holder[result]]
+
+        def give_bank(result):
+            free_banks.append(holder[result])
+            return banks[holder[result]]
+
+        def give_words(result):
+            return give_bank(result)[:].rearrange("p (t a) -> p a t", t=4)
+
+        def load_x(n):
+            nc.sync.dma_start(out=x_rows[n][:].rearrange("p (i k) -> p i k", i=2), in_=x[:, 2 * n : 2 * n + 2, :])
+
+        def load_weight(load):
+            w, g, h, count = load
+            rows = weights[w][GROUP * g : GROUP * (g + 1), GROUP * h : GROUP * (h + count)]
+            nc.sync.dma_start(
+                out=w_rows[load][:].rearrange("p (j c) -> p j c", j=4), in_=rows.rearrange("(p j) c -> p j c", j=4)
+            )
 
         def load_doc_words(c0, c1):
             cols = slice(2 * BANK * c0, 2 * BANK * c1)
             nc.sync.dma_start(
-                out=by_group(d_word[c0]).bitcast(I32),
+                out=by_group(doc_code[c0]).bitcast(I32),
                 in_=docs_words[:, :, cols].rearrange("g p n -> p g n").bitcast(I32),
             )
 
@@ -125,114 +131,119 @@ def tile_residual_query_maxsim_k1_kernel(
             cols = slice(BANK * c0, BANK * c1)
             for r in range(4):
                 nc.sync.dma_start(
-                    out=by_group(d_scale[c0])[r:P:32].bitcast(I32),
+                    out=by_group(doc_scale[c0])[r:P:32].bitcast(I32),
                     in_=docs_scales[:, r:16:4, cols].rearrange("g q n -> q g n").bitcast(I32),
                 )
 
-        def grouped(w, g, h):
-            return w_grp[w][g][h][:].rearrange("p (t m j) -> p t m j", t=4, j=4)
+        def loaded_piece(w, g, h):
+            load = [ld for ld in WEIGHT_LOADS if ld[:2] == (w, g) and ld[2] <= h < ld[2] + ld[3]][0]
+            rows = w_rows[load][:].rearrange("p (j c) -> p j c", j=4)
+            return rows[:, :, GROUP * (h - load[2]) : GROUP * (h - load[2] + 1)]
 
-        def weave(engine, w, g, h, t0, t1):
-            src = raw_piece(w, g, h).rearrange("p j (m t) -> p t m j", t=4)[:, t0:t1]
-            dst = grouped(w, g, h)[:, t0:t1]
-            if engine == "V":
-                nc.vector.tensor_copy(out=dst, in_=src)
-            else:
-                nc.scalar.copy(out=dst, in_=src)
+        def interleave_views(w, g, h, e):
+            src = loaded_piece(w, g, h).rearrange("p j (n s t) -> p n t s j", s=2, t=4)
+            dst = w_words[g, h][:].rearrange("p (t n s j) -> p n t s j", t=4, s=2, j=4)
+            return dst[:, :, 2 * e : 2 * e + 2], src[:, :, 2 * e : 2 * e + 2]
 
-        def weave_pe(w, g, h, e, b):
-            src = raw_piece(w, g, h).rearrange("p j (m t) -> p m t j", t=4)[:, :, 2 * e : 2 * e + 2, :]
-            dst = banks[b][:].bitcast(BF16).rearrange("p (t m j) -> p m t j", t=2, j=4)
+        def interleave_on_vector(w, g, h, e):
+            dst, src = interleave_views(w, g, h, e)
+            nc.vector.tensor_copy(out=dst, in_=src)
+
+        def interleave_on_scalar(w, g, h, e):
+            dst, src = interleave_views(w, g, h, e)
+            nc.scalar.copy(out=dst, in_=src)
+
+        def interleave_on_tensor(w, g, h, e):
+            src = loaded_piece(w, g, h).rearrange("p j (m t) -> p m t j", t=4)[:, :, 2 * e : 2 * e + 2, :]
+            dst = take_bank(("words", w, g, h))[:].bitcast(BF16).rearrange("p (t m j) -> p m t j", t=2, j=4)
             for s in range(2):
-                rows = slice(64 * s, 64 * (s + 1))
+                rows = slice(P // 2 * s, P // 2 * (s + 1))
                 nc.tensor.matmul(out=dst[:, rows], lhsT=ident16[:], rhs=src[:, rows], start=True, stop=True)
 
-        def weave_out(engine, w, g, h, e, b):
-            dst = half(w_grp[w][g][h], e)
-            src = banks[b][:].bitcast(BF16)
-            if engine == "V":
-                nc.vector.tensor_copy(out=dst, in_=src)
-            else:
-                nc.scalar.copy(out=dst, in_=src)
+        def copy_interleaved(w, g, h, e):
+            nc.scalar.copy(out=half(w_words[g, h], e), in_=give_bank(("words", w, g, h))[:].bitcast(BF16))
 
         def quantize(code, scale, src):
             nc.vector.quantize_mx(out=code.bitcast(FP8X4), scales=scale, in_=src)
 
         def quantize_w(w, g, h):
-            quantize(w_code[w][g][h][:], w_scale[w][g][h][:], w_grp[w][g][h][:])
+            quantize(w_code[w, g, h][:], w_scale[w, g, h][:], w_words[g, h][:])
 
-        def turn(b, slot, words):
+        def turn_group(bank, g, values):
+            pairs = values.bitcast(F32)
             for u in range(2):
-                col = (2 * slot + u) * P
-                nc.tensor.transpose(banks[b][:, col : col + P], words[:, u:256:2], ident[:])
+                col = (2 * g + u) * P
+                nc.tensor.transpose(bank[:, col : col + P], pairs[:, u : GROUP // 2 : 2], ident32[:])
 
-        def turn_x(i, b):
-            words = half(x_raw[i // 2], i % 2).bitcast(F32)
+        def turn_x(i):
+            bank = take_bank(("x", i))
             for g in range(G):
-                turn(b, g, words[:, 256 * g : 256 * (g + 1)])
+                turn_group(bank, g, half(x_rows[i // 2], i % 2)[:, GROUP * g : GROUP * (g + 1)])
 
-        def copy_x(i, b):
+        def copy_x(i):
             nc.scalar.copy(
-                out=x_t[i][:].bitcast(F32).rearrange("p (g a u) -> p g a u", g=G, u=2),
-                in_=banks[b][:].rearrange("p (g u a) -> p g a u", g=G, u=2),
+                out=x16[i][:].bitcast(F32).rearrange("p (g a u) -> p g a u", g=G, u=2),
+                in_=give_bank(("x", i))[:].rearrange("p (g u a) -> p g a u", g=G, u=2),
             )
 
-        def project(w, h, code, scale, b):
+        def quantize_x(i):
+            quantize(x_code[i][:], x_scale[i][:], x16[i][:])
+
+        def project(w, i, h, code, scale):
+            bank = take_bank((w, i, h))
             for t in range(4):
                 cols = slice(P * t, P * (t + 1))
                 for g in range(G):
                     nc.tensor.matmul_mx(
-                        out=banks[b][:, cols],
-                        lhsT=w_code[w][g][h][:, cols].bitcast(FP8X4),
-                        lhsT_scale=w_scale[w][g][h][:, cols],
+                        out=bank[:, cols],
+                        lhsT=w_code[w, g, h][:, cols].bitcast(FP8X4),
+                        lhsT_scale=w_scale[w, g, h][:, cols],
                         rhs=half(code, g).bitcast(FP8X4),
                         rhs_scale=half(scale, g),
                         start=(g == 0),
                         stop=(g == G - 1),
                     )
 
-        def stage1(i, h, b):
-            project(0, h, x_code[i], x_scale[i], b)
+        def adapt(i, h):
+            project(ADAPT, i, h, x_code[i], x_scale[i])
 
-        def stage2(i, h, b):
-            project(1, h, h_code[i], h_scale[i], b)
+        def proj(i, h):
+            project(PROJ, i, h, h_code[i], h_scale[i])
 
-        def h_on_vector(i, h, b):
+        def h_on_vector(i, h):
             nc.vector.scalar_tensor_tensor(
-                out=by_word(half(h32[i], h)), in0=bank_by_word(b), scalar=0.0,
-                in1=by_word(half(x_t[i], h)), op0=ALU.max, op1=ALU.add,
+                out=by_word(half(h32[i], h)),
+                in0=give_words((ADAPT, i, h)),
+                scalar=0.0,
+                in1=by_word(half(x16[i], h)),
+                op0=ALU.max,
+                op1=ALU.add,
             )
 
-        def r_on_vector(i, h, b):
+        def r_on_vector(i, h):
             nc.vector.tensor_tensor(
-                out=by_word(half(r16[i], h)), in0=bank_by_word(b), in1=by_word(half(h32[i], h)), op=ALU.add
+                out=by_word(half(r16[i], h)), in0=give_words((PROJ, i, h)), in1=by_word(half(h32[i], h)), op=ALU.add
             )
 
-        def relu_out(i, h, b):
-            nc.scalar.activation(out=by_word(half(z1[i], h)), in_=bank_by_word(b), func=ACT.Relu)
+        def relu_out(i, h):
+            nc.scalar.activation(out=by_word(half(relu32[i], h)), in_=give_words((ADAPT, i, h)), func=ACT.Relu)
 
-        def copy_out(i, h, b):
-            nc.scalar.copy(out=by_word(half(z2[i], h)), in_=bank_by_word(b))
+        def proj_out(i, h):
+            nc.scalar.copy(out=by_word(half(proj32[i], h)), in_=give_words((PROJ, i, h)))
 
-        def pool_op(dst, a, c, op, lo, hi):
-            for s in range(lo, hi, 256):
-                cols = slice(s, min(s + 256, hi))
-                nc.gpsimd.tensor_tensor(out=dst[:, cols], in0=a[:, cols], in1=c[:, cols], op=op)
+        def add_group_on_pool(dst, product, residual, h):
+            for start in range(GROUP * h, GROUP * (h + 1), POOL_PIECE):
+                cols = slice(start, start + POOL_PIECE)
+                nc.gpsimd.tensor_tensor(out=dst[:, cols], in0=product[:, cols], in1=residual[:, cols], op=ALU.add)
 
         def h_on_pool(i, h):
-            pool_op(h32[i], z1[i], x_t[i], ALU.add, 512 * h, 512 * (h + 1))
+            add_group_on_pool(h32[i], relu32[i], x16[i], h)
 
         def r_on_pool(i, h):
-            pool_op(r16[i], z2[i], h32[i], ALU.add, 512 * h, 512 * (h + 1))
+            add_group_on_pool(r16[i], proj32[i], h32[i], h)
 
         def round_h(i, h):
             nc.scalar.copy(out=half(h16[i], h), in_=half(h32[i], h))
-
-        def round_h_on_vector(i):
-            nc.vector.tensor_copy(out=h16[i][:], in_=h32[i][:])
-
-        def quantize_x(i):
-            quantize(x_code[i][:], x_scale[i][:], x_t[i][:])
 
         def quantize_h(i):
             quantize(h_code[i][:], h_scale[i][:], h16[i][:])
@@ -240,422 +251,191 @@ def tile_residual_query_maxsim_k1_kernel(
         def quantize_r(i):
             quantize(r_code[i][:], r_scale[i][:], r16[i][:])
 
-        def score(i, c, b):
+        def quantize_r_group(i, g):
+            quantize(half(r_code[i], g), half(r_scale[i], g), half(r16[i], g))
+
+        def chunk_of(tiles, loads, width, g, c):
+            c0 = [lo for lo, hi in loads if lo <= c < hi][0]
+            return by_group(tiles[c0])[:, g, width * (c - c0) : width * (c - c0 + 1)]
+
+        def score(n):
+            i, c = JOBS[n]
+            bank = take_bank(("score", n))
             for g in range(G):
                 nc.tensor.matmul_mx(
-                    out=banks[b][:],
+                    out=bank[:],
                     lhsT=half(r_code[i], g).bitcast(FP8X4),
                     lhsT_scale=half(r_scale[i], g),
-                    rhs=chunk_of(d_word, WORD_RUNS, 2 * BANK, g, c).bitcast(FP4X4),
-                    rhs_scale=chunk_of(d_scale, SCALE_RUNS, BANK, g, c),
+                    rhs=chunk_of(doc_code, WORD_LOADS, 2 * BANK, g, c).bitcast(FP4X4),
+                    rhs_scale=chunk_of(doc_scale, SCALE_LOADS, BANK, g, c),
                     start=(g == 0),
                     stop=(g == G - 1),
                 )
 
-        def reduce_max(i, c, b):
+        def maximum(n):
+            i, c = JOBS[n]
             nc.vector.tensor_reduce(
                 out=best[i][:, CHUNK_DOCS * c : CHUNK_DOCS * (c + 1)],
-                in_=banks[b][:].rearrange("p (d j) -> p d j", j=DTOK),
-                axis=AXIS_X,
+                in_=give_bank(("score", n))[:].rearrange("p (d j) -> p d j", j=DTOK),
+                axis=mybir.AxisListType.X,
                 op=ALU.max,
             )
 
-        def copy_upper(n, b):
-            nc.scalar.copy(
-                out=upper[n % 4][:].rearrange("p (d j) -> p d j", j=4),
-                in_=banks[b][:].rearrange("p (d j) -> p d j", j=DTOK)[:, :, 4:],
-            )
+        def add_best(engine, i, lo, hi):
+            so_far = best[0] if i == 1 else total
+            engine.tensor_tensor(out=total[:, lo:hi], in0=so_far[:, lo:hi], in1=best[i][:, lo:hi], op=ALU.add)
 
-        def max_to_four(n, q, s, b):
-            nc.vector.tensor_tensor(
-                out=four[q % 2][:, 256 * s : 256 * (s + 1)].rearrange("p (d j) -> p d j", j=4),
-                in0=banks[b][:].rearrange("p (d j) -> p d j", j=DTOK)[:, :, :4],
-                in1=upper[n % 4][:].rearrange("p (d j) -> p d j", j=4),
-                op=ALU.max,
-            )
-
-        def max_to_two(q, count):
-            src = four[q % 2][:, : 256 * count].rearrange("p (d j) -> p d j", j=4)
-            nc.vector.tensor_tensor(
-                out=two[q % 2][:, : 128 * count].rearrange("p (d j) -> p d j", j=2),
-                in0=src[:, :, :2], in1=src[:, :, 2:], op=ALU.max,
-            )
-
-        def max_to_one(q, count, i, c):
-            src = two[q % 2][:, : 128 * count].rearrange("p (d j) -> p d j", j=2)
-            nc.vector.tensor_tensor(
-                out=best[i][:, CHUNK_DOCS * c : CHUNK_DOCS * (c + count)],
-                in0=src[:, :, 0], in1=src[:, :, 1], op=ALU.max,
-            )
-
-        def add_on_pool(i, lo, hi):
-            first = best[0] if i == 1 else sum01
-            nc.gpsimd.tensor_tensor(out=sum01[:, lo:hi], in0=first[:, lo:hi], in1=best[i][:, lo:hi], op=ALU.add)
-
-        def weigh_on_pool(lo, hi):
-            nc.gpsimd.tensor_tensor(out=y32[:, lo:hi], in0=sum01[:, lo:hi], in1=d_weight[:, lo:hi], op=ALU.mult)
-
-        def add_on_vector(i, lo, hi):
-            first = best[0] if i == 1 else sum01
-            nc.vector.tensor_tensor(out=sum01[:, lo:hi], in0=first[:, lo:hi], in1=best[i][:, lo:hi], op=ALU.add)
-
-        def weigh(lo, hi):
-            nc.vector.tensor_tensor(out=y32[:, lo:hi], in0=sum01[:, lo:hi], in1=d_weight[:, lo:hi], op=ALU.mult)
-
-        def weigh_rounded(lo, hi):
-            nc.vector.tensor_tensor(out=y16[:, lo:hi], in0=sum01[:, lo:hi], in1=d_weight[:, lo:hi], op=ALU.mult)
-
-        def store_scales_of(g, q):
-            queue = nc.sync if q % 2 else nc.scalar
-            queue.dma_start(
-                out=out_2[g, 4 * q : 4 * q + 4, :].bitcast(I32),
-                in_=half(y_scale, g)[32 * q : 32 * q + 4, :].bitcast(I32),
-            )
-
-        def finish_on_pool(lo, hi):
-            pool_op(total, sum012, best[3], ALU.add, lo, hi)
-            pool_op(y32, total, d_weight, ALU.mult, lo, hi)
+        def weigh(engine, dst, lo, hi):
+            engine.tensor_tensor(out=dst[:, lo:hi], in0=total[:, lo:hi], in1=doc_gain[:, lo:hi], op=ALU.mult)
 
         def round_y(lo, hi):
             nc.scalar.copy(out=y16[:, lo:hi], in_=y32[:, lo:hi])
 
-        def add_best(i, lo, hi):
-            pool_op(sum01, best[0] if i == 1 else sum01, best[i], ALU.add, lo, hi)
+        def store_y(g):
+            nc.sync.dma_start(out=half(out_0, g), in_=half(y32, g))
 
-        def quantize_r_half(i, h):
-            quantize(half(r_code[i], h), half(r_scale[i], h), half(r16[i], h))
+        def turn_y(g):
+            turn_group(take_bank(("y", g)), 0, half(y16, g))
 
-        def round_h_vec(i, h):
-            nc.vector.tensor_copy(out=half(h16[i], h), in_=half(h32[i], h))
-
-        def round_h_pool(i, h):
-            nc.gpsimd.tensor_scalar(
-                out=half(h16[i], h), in0=half(h32[i], h), scalar1=1.0, scalar2=0.0, op0=ALU.mult, op1=ALU.add
-            )
-
-        def finish_on_vector(lo, hi):
-            last = slice(lo, hi)
-            nc.vector.tensor_tensor(out=total[:, last], in0=sum012[:, last], in1=best[3][:, last], op=ALU.add)
-            nc.vector.tensor_tensor(out=y16[:, last], in0=total[:, last], in1=d_weight[:, last], op=ALU.mult)
-            nc.vector.tensor_tensor(out=y32[:, last], in0=total[:, last], in1=d_weight[:, last], op=ALU.mult)
-
-        def load_weight_row():
-            nc.sync.dma_start(out=d_weight[:], in_=doc_weight.partition_broadcast(P))
-
-        def store_scales(q):
-            y_scale3 = y_scale[:].rearrange("p (g m) -> p g m", g=G)
-            queue = nc.sync if q % 2 else nc.scalar
-            queue.dma_start(
-                out=out_2[:, 4 * q : 4 * q + 4, :].rearrange("g r m -> r g m").bitcast(I32),
-                in_=y_scale3[32 * q : 32 * q + 4, :, :].bitcast(I32),
-            )
-
-        def setup(with_pe):
-            nc.vector.memset(warm_in[:], 0.0)
-            nc.scalar.activation(out=warm_out[:], in_=warm_in[:], func=ACT.Relu)
-            make_identity(nc, ident[:])
-            if with_pe:
-                make_identity(nc, ident16[:])
-            for c0, c1 in SCALE_RUNS:
-                nc.vector.memset(d_scale[c0][:].bitcast(I32), 0)
-
-        def store_y(lo, hi):
-            nc.sync.dma_start(out=out_0[:, lo:hi], in_=y32[:, lo:hi])
-
-        def turn_y(g, b):
-            turn(b, 0, half(y16, g).bitcast(F32))
-
-        def copy_y(g, b):
+        def copy_y(g):
             nc.scalar.copy(
-                out=half(y_t, g).bitcast(F32).rearrange("p (a u) -> p a u", u=2),
-                in_=banks[b][:, : 2 * P].rearrange("p (u a) -> p a u", u=2),
+                out=half(y_words, g).bitcast(F32).rearrange("p (a u) -> p a u", u=2),
+                in_=give_bank(("y", g))[:, : 2 * P].rearrange("p (u a) -> p a u", u=2),
             )
 
         def quantize_y(g):
-            quantize(half(y_code, g), half(y_scale, g), half(y_t, g))
+            quantize(half(y_code, g), half(y_scale, g), half(y_words, g))
 
-        def store_codes(g):
-            nc.sync.dma_start(
-                out=out_1[g].rearrange("p m t -> p (m t)").bitcast(I32), in_=half(y_code, g).bitcast(I32)
-            )
+        make_identity(nc, ident32[:])
+        nc.scalar.activation(out=ident16[:], in_=ident32[:], func=ACT.Relu)
+        for c0, c1 in SCALE_LOADS:
+            nc.vector.memset(doc_scale[c0][:].bitcast(I32), 0)
 
-        setup(1)
-        load_x(0)
-        load_w(0, 0, 0, 1)
-        load_x(1)
-        load_w(0, 0, 1, 1)
-        load_w(0, 1, 0, 2)
-        load_w(1, 0, 0, 2)
-        load_w(1, 1, 0, 1)
-        load_w(1, 1, 1, 1)
-        load_doc_scales(0, 8)
-        turn_x(0, 0)
-        turn_x(1, 1)
-        weave("S", 0, 0, 0, 2, 4)
-        weave("V", 0, 0, 0, 0, 2)
-        turn_x(2, 2)
-        copy_x(0, 0)
-        quantize_w(0, 0, 0)
-        turn_x(3, 3)
-        copy_x(1, 1)
-        weave("V", 0, 0, 1, 0, 2)
-        weave_pe(0, 0, 1, 1, 4)
-        copy_x(2, 2)
-        copy_x(3, 3)
+        for n in range(QTOK // 2):
+            load_x(n)
+        for load in WEIGHT_LOADS:
+            load_weight(load)
+        for s0, s1 in SCALE_LOADS:
+            load_doc_scales(s0, s1)
+            for c0, c1 in WORD_LOADS:
+                if s0 <= c0 < s1:
+                    load_doc_words(c0, c1)
+        nc.sync.dma_start(out=doc_gain[:], in_=doc_weight.partition_broadcast(P))
+
+        turn_x(0)
+        turn_x(1)
+        copy_x(0)
+        turn_x(2)
         quantize_x(0)
+        copy_x(1)
+        turn_x(3)
         quantize_x(1)
+        copy_x(2)
+        interleave_on_scalar(ADAPT, 0, 0, 1)
+        interleave_on_vector(ADAPT, 0, 1, 0)
+        interleave_on_tensor(ADAPT, 0, 1, 1)
+        interleave_on_vector(ADAPT, 0, 0, 0)
         quantize_x(2)
+        copy_x(3)
+        quantize_w(ADAPT, 0, 0)
+        interleave_on_scalar(ADAPT, 1, 0, 1)
+        interleave_on_tensor(ADAPT, 1, 1, 1)
+        interleave_on_vector(ADAPT, 1, 0, 0)
+        interleave_on_vector(ADAPT, 1, 1, 0)
+        copy_interleaved(ADAPT, 0, 1, 1)
+        quantize_w(ADAPT, 1, 0)
+        copy_interleaved(ADAPT, 1, 1, 1)
+
+        interleave_on_tensor(PROJ, 0, 0, 1)
+        quantize_w(ADAPT, 0, 1)
+        quantize_w(ADAPT, 1, 1)
+        adapt(0, 0)
+        interleave_on_scalar(PROJ, 0, 1, 0)
+        interleave_on_vector(PROJ, 0, 0, 0)
+        interleave_on_tensor(PROJ, 0, 1, 1)
+        interleave_on_vector(PROJ, 1, 0, 0)
+        adapt(0, 1)
+        copy_interleaved(PROJ, 0, 1, 1)
+        adapt(2, 0)
         quantize_x(3)
-        weave_out("S", 0, 0, 1, 1, 4)
-        load_doc_words(0, 2)
-        weave("V", 0, 1, 0, 0, 2)
-        weave_pe(0, 1, 1, 1, 5)
-        weave("S", 0, 1, 0, 2, 4)
-        quantize_w(0, 0, 1)
-        weave("V", 0, 1, 1, 0, 2)
-        weave_out("S", 0, 1, 1, 1, 5)
-        quantize_w(0, 1, 0)
-        load_doc_words(2, 4)
-        weave_pe(1, 0, 0, 1, 6)
-        weave("S", 1, 0, 1, 0, 2)
-        quantize_w(0, 1, 1)
-        stage1(0, 0, 7)
-        weave("V", 1, 0, 0, 0, 2)
-        stage1(0, 1, 0)
-        load_doc_words(4, 6)
-        weave_out("S", 1, 0, 0, 1, 6)
-        h_on_vector(0, 0, 7)
-        weave_pe(1, 1, 0, 1, 1)
-        h_on_vector(0, 1, 0)
-        round_h(0, 0)
-        stage1(1, 1, 2)
-        load_doc_words(6, 8)
-        quantize_w(1, 0, 0)
+        copy_interleaved(PROJ, 0, 0, 1)
+        h_on_vector(0, 1)
+        interleave_on_tensor(PROJ, 1, 0, 1)
+        h_on_vector(0, 0)
         round_h(0, 1)
-        weave_pe(1, 0, 1, 1, 3)
-        weave("V", 1, 1, 0, 0, 2)
-        load_doc_scales(8, 16)
-        weave_out("S", 1, 1, 0, 1, 1)
-        weave_pe(1, 1, 1, 1, 4)
+        adapt(2, 1)
+        interleave_on_vector(PROJ, 1, 1, 0)
+        round_h(0, 0)
+        interleave_on_tensor(PROJ, 1, 1, 1)
+        quantize_w(PROJ, 0, 0)
+        copy_interleaved(PROJ, 1, 0, 1)
+        adapt(1, 1)
         quantize_h(0)
-        weave("V", 1, 1, 1, 0, 2)
-        stage1(3, 0, 5)
-        weave_out("S", 1, 1, 1, 1, 4)
-        quantize_w(1, 1, 0)
-        stage1(2, 1, 6)
-        weave_out("S", 1, 0, 1, 1, 3)
-        quantize_w(1, 1, 1)
-        stage1(2, 0, 7)
-        relu_out(2, 1, 6)
-        quantize_w(1, 0, 1)
-        stage2(0, 0, 0)
-        h_on_vector(1, 1, 2)
+        copy_interleaved(PROJ, 1, 1, 1)
+        quantize_w(PROJ, 1, 0)
+        adapt(3, 0)
+        relu_out(2, 1)
+        quantize_w(PROJ, 0, 1)
+        proj(0, 0)
+        quantize_w(PROJ, 1, 1)
+        h_on_vector(1, 1)
         h_on_pool(2, 1)
-        stage2(0, 1, 1)
-        load_doc_words(8, 12)
-        r_on_vector(0, 0, 0)
+        proj(0, 1)
+        r_on_vector(0, 0)
         round_h(1, 1)
-        stage1(1, 0, 4)
-        r_on_vector(0, 1, 1)
-        relu_out(2, 0, 7)
-        stage1(3, 1, 3)
-        load_doc_words(12, 16)
-        quantize_r_half(0, 0)
-        quantize_r_half(0, 1)
-        round_h(2, 1)
-        h_on_vector(1, 0, 4)
-        score(0, 0, 6)
+        adapt(1, 0)
+        r_on_vector(0, 1)
+        relu_out(2, 0)
+        adapt(3, 1)
+        quantize_r_group(0, 0)
+        quantize_r_group(0, 1)
+        h_on_vector(1, 0)
         h_on_pool(2, 0)
-        score(0, 1, 2)
-        round_h(1, 0)
-        reduce_max(0, 0, 6)
-        load_weight_row()
-        score(0, 2, 0)
-        relu_out(3, 1, 3)
-        reduce_max(0, 1, 2)
-        score(0, 3, 1)
-        round_h(2, 0)
-        quantize_h(1)
-        score(0, 4, 7)
-        reduce_max(0, 2, 0)
-        h_on_pool(3, 1)
-        relu_out(3, 0, 5)
-        stage2(1, 1, 4)
-        quantize_h(2)
-        reduce_max(0, 3, 1)
-        stage2(1, 0, 6)
-        reduce_max(0, 4, 7)
-        score(0, 5, 3)
-        h_on_pool(3, 0)
-        round_h(3, 1)
-        r_on_vector(1, 0, 6)
-        stage2(2, 1, 2)
-        r_on_vector(1, 1, 4)
-        stage2(2, 0, 0)
-        quantize_r(1)
-        score(0, 6, 5)
-        round_h(3, 0)
-        reduce_max(0, 5, 3)
-        score(0, 7, 1)
-        copy_out(2, 0, 0)
-        quantize_h(3)
-        score(1, 0, 7)
-        reduce_max(0, 6, 5)
-        copy_out(2, 1, 2)
-        score(1, 1, 6)
-        reduce_max(0, 7, 1)
-        r_on_pool(2, 1)
-        score(1, 2, 4)
-        reduce_max(1, 0, 7)
-        score(1, 3, 3)
-        reduce_max(1, 1, 6)
-        stage2(3, 0, 0)
-        reduce_max(1, 2, 4)
-        r_on_pool(2, 0)
-        score(1, 4, 5)
-        reduce_max(1, 3, 3)
-        copy_out(3, 0, 0)
-        score(1, 5, 2)
-        reduce_max(1, 4, 5)
-        r_on_pool(3, 0)
-        score(1, 6, 1)
-        reduce_max(1, 5, 2)
-        score(1, 7, 7)
-        reduce_max(1, 6, 1)
-        score(0, 8, 6)
-        reduce_max(1, 7, 7)
-        score(0, 9, 4)
-        quantize_r(2)
-        score(0, 10, 3)
-        reduce_max(0, 8, 6)
-        add_on_pool(1, 0, 512)
-        score(0, 11, 0)
-        reduce_max(0, 9, 4)
-        score(2, 0, 5)
-        reduce_max(0, 10, 3)
-        score(2, 1, 2)
-        reduce_max(0, 11, 0)
-        score(2, 2, 1)
-        reduce_max(2, 0, 5)
-        score(2, 3, 7)
-        reduce_max(2, 1, 2)
-        stage2(3, 1, 6)
-        reduce_max(2, 2, 1)
-        score(2, 4, 4)
-        reduce_max(2, 3, 7)
-        copy_out(3, 1, 6)
-        score(2, 5, 3)
-        reduce_max(2, 4, 4)
-        r_on_pool(3, 1)
-        score(2, 6, 0)
-        reduce_max(2, 5, 3)
-        score(2, 7, 5)
-        reduce_max(2, 6, 0)
-        score(0, 12, 2)
-        reduce_max(2, 7, 5)
-        score(0, 13, 1)
-        quantize_r(3)
-        score(0, 14, 7)
-        reduce_max(0, 12, 2)
-        add_on_pool(2, 0, 512)
-        score(0, 15, 6)
-        reduce_max(0, 13, 1)
-        score(3, 0, 4)
-        reduce_max(0, 14, 7)
-        score(3, 1, 3)
-        reduce_max(0, 15, 6)
-        score(3, 2, 0)
-        reduce_max(3, 0, 4)
-        score(3, 3, 5)
-        reduce_max(3, 1, 3)
-        score(3, 4, 2)
-        reduce_max(3, 2, 0)
-        score(3, 5, 1)
-        reduce_max(3, 3, 5)
-        score(3, 6, 7)
-        reduce_max(3, 4, 2)
-        score(3, 7, 6)
-        reduce_max(3, 5, 1)
-        score(1, 8, 4)
-        reduce_max(3, 6, 7)
-        score(1, 9, 3)
-        reduce_max(3, 7, 6)
-        score(1, 10, 0)
-        reduce_max(1, 8, 4)
-        add_on_pool(3, 0, 512)
-        score(1, 11, 5)
-        reduce_max(1, 9, 3)
-        score(1, 12, 2)
-        reduce_max(1, 10, 0)
-        score(1, 13, 1)
-        reduce_max(1, 11, 5)
-        weigh_on_pool(0, 512)
-        score(1, 14, 7)
-        reduce_max(1, 12, 2)
-        score(1, 15, 6)
-        reduce_max(1, 13, 1)
-        score(2, 8, 4)
-        reduce_max(1, 14, 7)
-        store_y(0, 512)
-        round_y(0, 512)
-        score(2, 9, 3)
-        reduce_max(1, 15, 6)
-        score(2, 10, 0)
-        reduce_max(2, 8, 4)
-        add_on_pool(1, 512, 1024)
-        score(2, 11, 5)
-        reduce_max(2, 9, 3)
-        score(2, 12, 2)
-        reduce_max(2, 10, 0)
-        turn_y(0, 1)
-        reduce_max(2, 11, 5)
-        score(2, 13, 7)
-        copy_y(0, 1)
-        reduce_max(2, 12, 2)
-        score(2, 14, 6)
-        reduce_max(2, 13, 7)
-        score(2, 15, 4)
-        reduce_max(2, 14, 6)
-        score(3, 8, 3)
-        reduce_max(2, 15, 4)
-        score(3, 9, 0)
-        reduce_max(3, 8, 3)
-        add_on_pool(2, 512, 1024)
-        score(3, 10, 5)
-        reduce_max(3, 9, 0)
-        score(3, 11, 1)
-        reduce_max(3, 10, 5)
-        score(3, 12, 2)
-        reduce_max(3, 11, 1)
-        score(3, 13, 7)
-        add_on_pool(3, 512, 704)
-        reduce_max(3, 12, 2)
-        score(3, 14, 6)
-        reduce_max(3, 13, 7)
-        score(3, 15, 4)
-        add_on_pool(3, 704, 832)
-        reduce_max(3, 14, 6)
-        weigh_on_pool(512, 704)
-        reduce_max(3, 15, 4)
-        weigh_on_pool(704, 832)
-        round_y(512, 704)
+
+        mid = DOCS // 2
+        behind = {
+            1: [(round_h, 1, 0), (relu_out, 3, 1), (quantize_h, 1), (h_on_pool, 3, 1)],
+            3: [(round_h, 2, 0), (round_h, 2, 1), (relu_out, 3, 0)],
+            4: [(proj, 1, 1), (proj, 1, 0), (quantize_h, 2), (r_on_vector, 1, 1), (h_on_pool, 3, 0), (r_on_vector, 1, 0)],
+            5: [(proj, 2, 1), (proj_out, 2, 1), (quantize_r, 1), (round_h, 3, 0), (r_on_pool, 2, 1)],
+            7: [(proj, 2, 0), (round_h, 3, 1), (proj_out, 2, 0)],
+            8: [(quantize_h, 3), (r_on_pool, 2, 0)],
+            13: [(proj, 3, 0), (quantize_r, 2), (proj_out, 3, 0), (r_on_pool, 3, 0)],
+            16: [(add_best, nc.gpsimd, 1, 0, mid)],
+            24: [(add_best, nc.gpsimd, 2, 0, mid)],
+            30: [(proj, 3, 1), (proj_out, 3, 1), (r_on_pool, 3, 1)],
+            37: [(quantize_r, 3)],
+            40: [(add_best, nc.gpsimd, 1, mid, DOCS)],
+            48: [(add_best, nc.gpsimd, 3, 0, mid), (weigh, nc.gpsimd, y32, 0, mid), (store_y, 0), (round_y, 0, mid)],
+            56: [(add_best, nc.gpsimd, 2, mid, DOCS)],
+            59: [(add_best, nc.gpsimd, 3, mid, POOL_END), (weigh, nc.gpsimd, y32, mid, POOL_END)],
+        }
+        score(0)
+        for n in range(1, len(JOBS)):
+            score(n)
+            maximum(n - 1)
+            for step in behind.get(n, []):
+                step[0](*step[1:])
+
+        turn_y(0)
+        maximum(len(JOBS) - 1)
+        copy_y(0)
+        add_best(nc.vector, 3, POOL_END, DOCS)
+        round_y(mid, POOL_END)
+        weigh(nc.vector, y16, POOL_END, DOCS)
+        weigh(nc.vector, y32, POOL_END, DOCS)
+        turn_y(1)
         quantize_y(0)
-        add_on_vector(3, 832, 1024)
-        store_scales_of(0, 3)
-        store_scales_of(0, 2)
-        store_codes(0)
-        store_scales_of(0, 0)
-        store_scales_of(0, 1)
-        round_y(704, 832)
-        weigh_rounded(832, 1024)
-        store_y(512, 832)
-        weigh(832, 1024)
-        turn_y(1, 3)
-        store_y(832, 1024)
-        copy_y(1, 3)
+        store_y(1)
+        copy_y(1)
         quantize_y(1)
-        store_codes(1)
-        store_scales_of(1, 0)
-        store_scales_of(1, 1)
-        store_scales_of(1, 2)
-        store_scales_of(1, 3)
+
+        nc.sync.dma_start(
+            out=out_1.rearrange("g p m t -> p g (m t)").bitcast(I32), in_=by_group(y_code).bitcast(I32)
+        )
+        for q in range(4):
+            queue = nc.sync if q % 2 else nc.scalar
+            queue.dma_start(
+                out=out_2[:, 4 * q : 4 * q + 4, :].rearrange("g r m -> r g m").bitcast(I32),
+                in_=by_group(y_scale)[32 * q : 32 * q + 4].bitcast(I32),
+            )

from contextlib import ExitStack

import concourse.mybir as mybir
from concourse.masks import make_identity

F32 = mybir.dt.float32
BF16 = mybir.dt.bfloat16
I32 = mybir.dt.int32
U32 = mybir.dt.uint32
U8 = mybir.dt.uint8
FP8X4 = mybir.dt.float8_e4m3fn_x4
FP4X4 = mybir.dt.float4_e2m1fn_x4
ALU = mybir.AluOpType
ACT = mybir.ActivationFunctionType

P = 128
QTOK, DOCS, DTOK, K = 4, 1024, 8, 1024
GROUP = 512
G = K // GROUP
BANK = 512
BANKS = 8
CHUNK_DOCS = BANK // DTOK
CHUNKS = DOCS // CHUNK_DOCS
HALF_CHUNKS = CHUNKS // 2
ADAPT, PROJ = 0, 1

FLOPS = 2 * P * QTOK * K * (K + K + DOCS * DTOK)

WEIGHT_LOADS = [(ADAPT, 0, 0, 2), (ADAPT, 1, 0, 2), (PROJ, 0, 0, 2), (PROJ, 1, 0, 1), (PROJ, 1, 1, 1)]
WORD_LOADS = [(0, 2), (2, 4), (4, 6), (6, 8), (8, 12), (12, 16)]
SCALE_LOADS = [(0, HALF_CHUNKS), (HALF_CHUNKS, CHUNKS)]

SWEEPS = [(0, 0), (1, 0), (2, 0), (0, 1), (1, 1), (3, 0), (2, 1), (3, 1)]
JOBS = [(i, HALF_CHUNKS * s + c) for i, s in SWEEPS for c in range(HALF_CHUNKS)]

POOL_TILES = (2, 3)
POOL_PIECE = 256
POOL_END = 704


def tile_residual_query_maxsim_k1_kernel(
    tc, x, w_adapt, w_proj, docs_words, docs_scales, doc_weight, out_0, out_1, out_2
):
    nc = tc.nc
    weights = (w_adapt, w_proj)
    with ExitStack() as ctx:
        sb = ctx.enter_context(tc.tile_pool(name="sb", bufs=1))
        ps = ctx.enter_context(tc.psum_pool(name="ps", bufs=1))
        ctx.enter_context(tc.manual_schedule())

        def keep(name, width, dtype):
            return sb.tile([P, width], dtype, name=name, align_bytes=64)

        def per_tile(name, width, dtype, tiles):
            return {i: keep("%s%d" % (name, i), width, dtype) for i in tiles}

        pieces = [(w, g, h) for w in (ADAPT, PROJ) for g in range(G) for h in range(G)]
        banks = [ps.tile([P, BANK], F32, name="bank%d" % b) for b in range(BANKS)]
        ident32 = keep("ident32", P, F32)
        ident16 = keep("ident16", P, BF16)
        w_rows = {load: keep("w_rows%d%d%d" % load[:3], 4 * GROUP * load[3], BF16) for load in WEIGHT_LOADS}
        w_words = {(g, h): keep("w_words%d%d" % (g, h), 4 * GROUP, BF16) for g in range(G) for h in range(G)}
        w_code = {piece: keep("w_code%d%d%d" % piece, GROUP, U32) for piece in pieces}
        w_scale = {piece: keep("w_scale%d%d%d" % piece, GROUP, U8) for piece in pieces}
        x_rows = per_tile("x_rows", 2 * K, BF16, range(QTOK // 2))
        x16 = per_tile("x16_", K, BF16, range(QTOK))
        h32 = per_tile("h32_", K, F32, range(QTOK))
        h16 = per_tile("h16_", K, BF16, range(QTOK))
        r16 = per_tile("r16_", K, BF16, range(QTOK))
        relu32 = per_tile("relu32_", K, F32, POOL_TILES)
        proj32 = per_tile("proj32_", K, F32, POOL_TILES)
        x_code = per_tile("x_code", G * P, U32, range(QTOK))
        x_scale = per_tile("x_scale", G * P, U8, range(QTOK))
        h_code = per_tile("h_code", G * P, U32, range(QTOK))
        h_scale = per_tile("h_scale", G * P, U8, range(QTOK))
        r_code = per_tile("r_code", G * P, U32, range(QTOK))
        r_scale = per_tile("r_scale", G * P, U8, range(QTOK))
        doc_code = {c0: keep("doc_code%d" % c0, G * 2 * BANK * (c1 - c0), U8) for c0, c1 in WORD_LOADS}
        doc_scale = {c0: keep("doc_scale%d" % c0, G * BANK * (c1 - c0), U8) for c0, c1 in SCALE_LOADS}
        doc_gain = keep("doc_gain", DOCS, BF16)
        best = per_tile("best", DOCS, F32, range(QTOK))
        total = keep("total", DOCS, F32)
        y32 = keep("y32", DOCS, F32)
        y16 = keep("y16", DOCS, BF16)
        y_words = keep("y_words", DOCS, BF16)
        y_code = keep("y_code", G * P, U32)
        y_scale = keep("y_scale", G * P, U8)

        def half(tile, n):
            width = tile.shape[1] // 2
            return tile[:, n * width : (n + 1) * width]

        def by_group(tile):
            return tile[:].rearrange("p (g n) -> p g n", g=G)

        def by_word(ap):
            return ap.rearrange("p (a t) -> p a t", t=4)

        free_banks = list(range(BANKS))
        holder = {}

        def take_bank(result):
            holder[result] = free_banks.pop(0)
            return banks[holder[result]]

        def give_bank(result):
            free_banks.append(holder[result])
            return banks[holder[result]]

        def give_words(result):
            return give_bank(result)[:].rearrange("p (t a) -> p a t", t=4)

        def load_x(n):
            nc.sync.dma_start(out=x_rows[n][:].rearrange("p (i k) -> p i k", i=2), in_=x[:, 2 * n : 2 * n + 2, :])

        def load_weight(load):
            w, g, h, count = load
            rows = weights[w][GROUP * g : GROUP * (g + 1), GROUP * h : GROUP * (h + count)]
            nc.sync.dma_start(
                out=w_rows[load][:].rearrange("p (j c) -> p j c", j=4), in_=rows.rearrange("(p j) c -> p j c", j=4)
            )

        def load_doc_words(c0, c1):
            cols = slice(2 * BANK * c0, 2 * BANK * c1)
            nc.sync.dma_start(
                out=by_group(doc_code[c0]).bitcast(I32),
                in_=docs_words[:, :, cols].rearrange("g p n -> p g n").bitcast(I32),
            )

        def load_doc_scales(c0, c1):
            cols = slice(BANK * c0, BANK * c1)
            for r in range(4):
                nc.sync.dma_start(
                    out=by_group(doc_scale[c0])[r:P:32].bitcast(I32),
                    in_=docs_scales[:, r:16:4, cols].rearrange("g q n -> q g n").bitcast(I32),
                )

        def loaded_piece(w, g, h):
            load = [ld for ld in WEIGHT_LOADS if ld[:2] == (w, g) and ld[2] <= h < ld[2] + ld[3]][0]
            rows = w_rows[load][:].rearrange("p (j c) -> p j c", j=4)
            return rows[:, :, GROUP * (h - load[2]) : GROUP * (h - load[2] + 1)]

        def interleave_views(w, g, h, e):
            src = loaded_piece(w, g, h).rearrange("p j (n s t) -> p n t s j", s=2, t=4)
            dst = w_words[g, h][:].rearrange("p (t n s j) -> p n t s j", t=4, s=2, j=4)
            return dst[:, :, 2 * e : 2 * e + 2], src[:, :, 2 * e : 2 * e + 2]

        def interleave_on_vector(w, g, h, e):
            dst, src = interleave_views(w, g, h, e)
            nc.vector.tensor_copy(out=dst, in_=src)

        def interleave_on_scalar(w, g, h, e):
            dst, src = interleave_views(w, g, h, e)
            nc.scalar.copy(out=dst, in_=src)

        def interleave_on_tensor(w, g, h, e):
            src = loaded_piece(w, g, h).rearrange("p j (m t) -> p m t j", t=4)[:, :, 2 * e : 2 * e + 2, :]
            dst = take_bank(("words", w, g, h))[:].bitcast(BF16).rearrange("p (t m j) -> p m t j", t=2, j=4)
            for s in range(2):
                rows = slice(P // 2 * s, P // 2 * (s + 1))
                nc.tensor.matmul(out=dst[:, rows], lhsT=ident16[:], rhs=src[:, rows], start=True, stop=True)

        def copy_interleaved(w, g, h, e):
            nc.scalar.copy(out=half(w_words[g, h], e), in_=give_bank(("words", w, g, h))[:].bitcast(BF16))

        def quantize(code, scale, src):
            nc.vector.quantize_mx(out=code.bitcast(FP8X4), scales=scale, in_=src)

        def quantize_w(w, g, h):
            quantize(w_code[w, g, h][:], w_scale[w, g, h][:], w_words[g, h][:])

        def turn_group(bank, g, values):
            pairs = values.bitcast(F32)
            for u in range(2):
                col = (2 * g + u) * P
                nc.tensor.transpose(bank[:, col : col + P], pairs[:, u : GROUP // 2 : 2], ident32[:])

        def turn_x(i):
            bank = take_bank(("x", i))
            for g in range(G):
                turn_group(bank, g, half(x_rows[i // 2], i % 2)[:, GROUP * g : GROUP * (g + 1)])

        def copy_x(i):
            nc.scalar.copy(
                out=x16[i][:].bitcast(F32).rearrange("p (g a u) -> p g a u", g=G, u=2),
                in_=give_bank(("x", i))[:].rearrange("p (g u a) -> p g a u", g=G, u=2),
            )

        def quantize_x(i):
            quantize(x_code[i][:], x_scale[i][:], x16[i][:])

        def project(w, i, h, code, scale):
            bank = take_bank((w, i, h))
            for t in range(4):
                cols = slice(P * t, P * (t + 1))
                for g in range(G):
                    nc.tensor.matmul_mx(
                        out=bank[:, cols],
                        lhsT=w_code[w, g, h][:, cols].bitcast(FP8X4),
                        lhsT_scale=w_scale[w, g, h][:, cols],
                        rhs=half(code, g).bitcast(FP8X4),
                        rhs_scale=half(scale, g),
                        start=(g == 0),
                        stop=(g == G - 1),
                    )

        def adapt(i, h):
            project(ADAPT, i, h, x_code[i], x_scale[i])

        def proj(i, h):
            project(PROJ, i, h, h_code[i], h_scale[i])

        def h_on_vector(i, h):
            nc.vector.scalar_tensor_tensor(
                out=by_word(half(h32[i], h)),
                in0=give_words((ADAPT, i, h)),
                scalar=0.0,
                in1=by_word(half(x16[i], h)),
                op0=ALU.max,
                op1=ALU.add,
            )

        def r_on_vector(i, h):
            nc.vector.tensor_tensor(
                out=by_word(half(r16[i], h)), in0=give_words((PROJ, i, h)), in1=by_word(half(h32[i], h)), op=ALU.add
            )

        def relu_out(i, h):
            nc.scalar.activation(out=by_word(half(relu32[i], h)), in_=give_words((ADAPT, i, h)), func=ACT.Relu)

        def proj_out(i, h):
            nc.scalar.copy(out=by_word(half(proj32[i], h)), in_=give_words((PROJ, i, h)))

        def add_group_on_pool(dst, product, residual, h):
            for start in range(GROUP * h, GROUP * (h + 1), POOL_PIECE):
                cols = slice(start, start + POOL_PIECE)
                nc.gpsimd.tensor_tensor(out=dst[:, cols], in0=product[:, cols], in1=residual[:, cols], op=ALU.add)

        def h_on_pool(i, h):
            add_group_on_pool(h32[i], relu32[i], x16[i], h)

        def r_on_pool(i, h):
            add_group_on_pool(r16[i], proj32[i], h32[i], h)

        def round_h(i, h):
            nc.scalar.copy(out=half(h16[i], h), in_=half(h32[i], h))

        def quantize_h(i):
            quantize(h_code[i][:], h_scale[i][:], h16[i][:])

        def quantize_r(i):
            quantize(r_code[i][:], r_scale[i][:], r16[i][:])

        def quantize_r_group(i, g):
            quantize(half(r_code[i], g), half(r_scale[i], g), half(r16[i], g))

        def chunk_of(tiles, loads, width, g, c):
            c0 = [lo for lo, hi in loads if lo <= c < hi][0]
            return by_group(tiles[c0])[:, g, width * (c - c0) : width * (c - c0 + 1)]

        def score(n):
            i, c = JOBS[n]
            bank = take_bank(("score", n))
            for g in range(G):
                nc.tensor.matmul_mx(
                    out=bank[:],
                    lhsT=half(r_code[i], g).bitcast(FP8X4),
                    lhsT_scale=half(r_scale[i], g),
                    rhs=chunk_of(doc_code, WORD_LOADS, 2 * BANK, g, c).bitcast(FP4X4),
                    rhs_scale=chunk_of(doc_scale, SCALE_LOADS, BANK, g, c),
                    start=(g == 0),
                    stop=(g == G - 1),
                )

        def maximum(n):
            i, c = JOBS[n]
            nc.vector.tensor_reduce(
                out=best[i][:, CHUNK_DOCS * c : CHUNK_DOCS * (c + 1)],
                in_=give_bank(("score", n))[:].rearrange("p (d j) -> p d j", j=DTOK),
                axis=mybir.AxisListType.X,
                op=ALU.max,
            )

        def add_best(engine, i, lo, hi):
            so_far = best[0] if i == 1 else total
            engine.tensor_tensor(out=total[:, lo:hi], in0=so_far[:, lo:hi], in1=best[i][:, lo:hi], op=ALU.add)

        def weigh(engine, dst, lo, hi):
            engine.tensor_tensor(out=dst[:, lo:hi], in0=total[:, lo:hi], in1=doc_gain[:, lo:hi], op=ALU.mult)

        def round_y(lo, hi):
            nc.scalar.copy(out=y16[:, lo:hi], in_=y32[:, lo:hi])

        def store_y(g):
            nc.sync.dma_start(out=half(out_0, g), in_=half(y32, g))

        def turn_y(g):
            turn_group(take_bank(("y", g)), 0, half(y16, g))

        def copy_y(g):
            nc.scalar.copy(
                out=half(y_words, g).bitcast(F32).rearrange("p (a u) -> p a u", u=2),
                in_=give_bank(("y", g))[:, : 2 * P].rearrange("p (u a) -> p a u", u=2),
            )

        def quantize_y(g):
            quantize(half(y_code, g), half(y_scale, g), half(y_words, g))

        make_identity(nc, ident32[:])
        nc.scalar.activation(out=ident16[:], in_=ident32[:], func=ACT.Relu)
        for c0, c1 in SCALE_LOADS:
            nc.vector.memset(doc_scale[c0][:].bitcast(I32), 0)

        for n in range(QTOK // 2):
            load_x(n)
        for load in WEIGHT_LOADS:
            load_weight(load)
        for s0, s1 in SCALE_LOADS:
            load_doc_scales(s0, s1)
            for c0, c1 in WORD_LOADS:
                if s0 <= c0 < s1:
                    load_doc_words(c0, c1)
        nc.sync.dma_start(out=doc_gain[:], in_=doc_weight.partition_broadcast(P))

        turn_x(0)
        turn_x(1)
        copy_x(0)
        turn_x(2)
        quantize_x(0)
        copy_x(1)
        turn_x(3)
        quantize_x(1)
        copy_x(2)
        interleave_on_scalar(ADAPT, 0, 0, 1)
        interleave_on_vector(ADAPT, 0, 1, 0)
        interleave_on_tensor(ADAPT, 0, 1, 1)
        interleave_on_vector(ADAPT, 0, 0, 0)
        quantize_x(2)
        copy_x(3)
        quantize_w(ADAPT, 0, 0)
        interleave_on_scalar(ADAPT, 1, 0, 1)
        interleave_on_tensor(ADAPT, 1, 1, 1)
        interleave_on_vector(ADAPT, 1, 0, 0)
        interleave_on_vector(ADAPT, 1, 1, 0)
        copy_interleaved(ADAPT, 0, 1, 1)
        quantize_w(ADAPT, 1, 0)
        copy_interleaved(ADAPT, 1, 1, 1)

        interleave_on_tensor(PROJ, 0, 0, 1)
        quantize_w(ADAPT, 0, 1)
        quantize_w(ADAPT, 1, 1)
        adapt(0, 0)
        interleave_on_scalar(PROJ, 0, 1, 0)
        interleave_on_vector(PROJ, 0, 0, 0)
        interleave_on_tensor(PROJ, 0, 1, 1)
        interleave_on_vector(PROJ, 1, 0, 0)
        adapt(0, 1)
        copy_interleaved(PROJ, 0, 1, 1)
        adapt(2, 0)
        quantize_x(3)
        copy_interleaved(PROJ, 0, 0, 1)
        h_on_vector(0, 1)
        interleave_on_tensor(PROJ, 1, 0, 1)
        h_on_vector(0, 0)
        round_h(0, 1)
        adapt(2, 1)
        interleave_on_vector(PROJ, 1, 1, 0)
        round_h(0, 0)
        interleave_on_tensor(PROJ, 1, 1, 1)
        quantize_w(PROJ, 0, 0)
        copy_interleaved(PROJ, 1, 0, 1)
        adapt(1, 1)
        quantize_h(0)
        copy_interleaved(PROJ, 1, 1, 1)
        quantize_w(PROJ, 1, 0)
        adapt(3, 0)
        relu_out(2, 1)
        quantize_w(PROJ, 0, 1)
        proj(0, 0)
        quantize_w(PROJ, 1, 1)
        h_on_vector(1, 1)
        h_on_pool(2, 1)
        proj(0, 1)
        r_on_vector(0, 0)
        round_h(1, 1)
        adapt(1, 0)
        r_on_vector(0, 1)
        relu_out(2, 0)
        adapt(3, 1)
        quantize_r_group(0, 0)
        quantize_r_group(0, 1)
        h_on_vector(1, 0)
        h_on_pool(2, 0)

        mid = DOCS // 2
        behind = {
            1: [(round_h, 1, 0), (relu_out, 3, 1), (quantize_h, 1), (h_on_pool, 3, 1)],
            3: [(round_h, 2, 0), (round_h, 2, 1), (relu_out, 3, 0)],
            4: [(proj, 1, 1), (proj, 1, 0), (quantize_h, 2), (r_on_vector, 1, 1), (h_on_pool, 3, 0), (r_on_vector, 1, 0)],
            5: [(proj, 2, 1), (proj_out, 2, 1), (quantize_r, 1), (round_h, 3, 0), (r_on_pool, 2, 1)],
            7: [(proj, 2, 0), (round_h, 3, 1), (proj_out, 2, 0)],
            8: [(quantize_h, 3), (r_on_pool, 2, 0)],
            13: [(proj, 3, 0), (quantize_r, 2), (proj_out, 3, 0), (r_on_pool, 3, 0)],
            16: [(add_best, nc.gpsimd, 1, 0, mid)],
            24: [(add_best, nc.gpsimd, 2, 0, mid)],
            30: [(proj, 3, 1), (proj_out, 3, 1), (r_on_pool, 3, 1)],
            37: [(quantize_r, 3)],
            40: [(add_best, nc.gpsimd, 1, mid, DOCS)],
            48: [(add_best, nc.gpsimd, 3, 0, mid), (weigh, nc.gpsimd, y32, 0, mid), (store_y, 0), (round_y, 0, mid)],
            56: [(add_best, nc.gpsimd, 2, mid, DOCS)],
            59: [(add_best, nc.gpsimd, 3, mid, POOL_END), (weigh, nc.gpsimd, y32, mid, POOL_END)],
        }
        score(0)
        for n in range(1, len(JOBS)):
            score(n)
            maximum(n - 1)
            for step in behind.get(n, []):
                step[0](*step[1:])

        turn_y(0)
        maximum(len(JOBS) - 1)
        copy_y(0)
        add_best(nc.vector, 3, POOL_END, DOCS)
        round_y(mid, POOL_END)
        weigh(nc.vector, y16, POOL_END, DOCS)
        weigh(nc.vector, y32, POOL_END, DOCS)
        turn_y(1)
        quantize_y(0)
        store_y(1)
        copy_y(1)
        quantize_y(1)

        nc.sync.dma_start(
            out=out_1.rearrange("g p m t -> p g (m t)").bitcast(I32), in_=by_group(y_code).bitcast(I32)
        )
        for q in range(4):
            queue = nc.sync if q % 2 else nc.scalar
            queue.dma_start(
                out=out_2[:, 4 * q : 4 * q + 4, :].rearrange("g r m -> r g m").bitcast(I32),
                in_=by_group(y_scale)[32 * q : 32 * q + 4].bitcast(I32),
            )
